import numpy as np
import ml_dtypes


def mxq(x, axis, fmt="e4m3"):
    dtype, down = {"e4m3": (ml_dtypes.float8_e4m3fn, 7), "e5m2": (ml_dtypes.float8_e5m2, 14)}[fmt]
    v = np.moveaxis(np.asarray(x, np.float32).astype(ml_dtypes.bfloat16).astype(np.float64), axis, -1)
    blocks = v.reshape(v.shape[:-1] + (-1, 32))
    amax = np.abs(blocks).max(-1, keepdims=True)
    byte = np.maximum(np.where(amax > 0, np.frexp(amax)[1] - 1 + 127, 0) - down, 1)
    scale = np.exp2(byte - 127.0)
    codes = (blocks / scale).astype(np.float32).astype(dtype).astype(np.float64)
    return np.moveaxis((codes * scale).reshape(v.shape), -1, axis)


WIDE = False


def mx_kscale(k):
    if not WIDE:
        return np.ones(k)
    levels = np.array([10, -10, 5, -5, 0])
    if k % 512:
        return np.exp2(np.random.permutation(np.resize(levels, k // 32))).repeat(32)
    a = np.empty((k // 512, 16))
    for p in range(k // 512):
        a[p, :8] = np.random.permutation(np.resize(levels, 8))
        for g in range(8):
            far = levels[np.abs(levels - a[p, g]) >= 10]
            a[p, g + 8] = far[np.random.randint(len(far))]
    return np.exp2(a.ravel()).repeat(32)


def f64(x):
    return np.asarray(x).astype(np.float64)


def striped(idx):
    return np.tile(idx.reshape(-1, 16).T, (8, 1)).astype(np.uint16)


def unstriped(offs):
    return offs[:16].T.reshape(-1).astype(np.int64)


E2M1 = np.array([0.0, 0.5, 1.0, 1.5, 2.0, 3.0, 4.0, 6.0, -0.0, -0.5, -1.0, -1.5, -2.0, -3.0, -4.0, -6.0])


def pack_weight(w, fmt):
    k, n = w.shape
    w = f64(np.asarray(w, np.float32).astype(ml_dtypes.bfloat16)).reshape(k // 32, 32, n)
    amax = np.abs(w).max(1)
    if fmt == "e4m3":
        byte = np.frexp(amax)[1] - 1 + 127 - 7
    else:
        mant, ex = np.frexp(amax / 6.0)
        byte = np.where(mant > 0.5, ex, ex - 1) + 127
    byte = np.clip(np.where(amax > 0, byte, 1), 1, 254)
    scaled = (w * np.exp2(127.0 - byte)[:, None, :]).reshape(k, n).astype(np.float32)
    by_word = np.ascontiguousarray(scaled.reshape(k // 512, 128, 4, n).transpose(0, 1, 3, 2))
    if fmt == "e4m3":
        words = by_word.astype(ml_dtypes.float8_e4m3fn).view(np.uint8)
    else:
        c = by_word.astype(ml_dtypes.float4_e2m1fn).view(np.uint8) & 0xF
        words = (c[..., 0::2] | (c[..., 1::2] << 4)).reshape(k // 512, 128, 2 * n)
    return np.ascontiguousarray(words), np.ascontiguousarray(byte.astype(np.uint8).reshape(k // 512, 16, n))


def unpack_weight(words, scales, fmt):
    g, _, n = scales.shape
    words = np.ascontiguousarray(words).reshape(g, 128, n, -1)
    if fmt == "e4m3":
        vals = words.view(ml_dtypes.float8_e4m3fn).astype(np.float64)
    else:
        nib = np.empty((g, 128, n, 4), np.uint8)
        nib[..., 0::2] = words & 0xF
        nib[..., 1::2] = words >> 4
        vals = E2M1[nib]
    vals = vals * np.repeat(np.exp2(scales.astype(np.float64) - 127.0), 8, axis=1)[..., None]
    return vals.transpose(0, 1, 3, 2).reshape(g * 512, n)


def relu(v):
    return np.maximum(v, 0.0)


K, T, E, C, H, N = 512, 512, 8, 128, 512, 128


def by_expert(wq, xq):
    return np.concatenate([wq[e].T @ xq[:, e * C:(e + 1) * C] for e in range(E)], axis=1)


def setup_inputs():
    n = np.random.standard_normal
    s = mx_kscale(K)
    u = mx_kscale(H)
    first = np.random.permutation(np.repeat(np.arange(E), T // E))
    second = (first + 1 + np.random.permutation(np.repeat(np.arange(E - 1), -(-T // (E - 1)))[:T])) % E
    while np.bincount(second, minlength=E).max() != T // E:
        load = np.bincount(second, minlength=E); hi, lo = int(load.argmax()), int(load.argmin())
        t = np.flatnonzero((second == hi) & (first != lo))[0]; second[t] = lo
    slot_token = np.empty(E * C, np.int64); pos = np.empty((2, T), np.int64); fill = np.zeros(E, np.int64)
    place = np.stack([np.random.permutation(C) for _ in range(E)])
    for r, deal in enumerate((first, second)):
        for t in np.random.permutation(T):
            e = deal[t]; j = e * C + place[e, fill[e]]; fill[e] += 1; slot_token[j] = t; pos[r, t] = j
    g = np.random.uniform(0.2, 0.8, T)
    x = pack_weight(n((K, T)) * s[:, None], "e4m3")
    w1 = [pack_weight(m, "e2m1") for m in n((E, K, H)) / np.sqrt(K) / s[None, :, None]]
    w3 = [pack_weight(m, "e2m1") for m in n((E, K, H)) / np.sqrt(K) / s[None, :, None] * u]
    w2 = pack_weight(n((H, N)) / np.sqrt(H) / u[:, None], "e4m3")
    return {
        "x_words": x[0],
        "x_scales": x[1],
        "w1_words": np.stack([m[0] for m in w1]),
        "w1_scales": np.stack([m[1] for m in w1]),
        "w3_words": np.stack([m[0] for m in w3]),
        "w3_scales": np.stack([m[1] for m in w3]),
        "w2_words": w2[0],
        "w2_scales": w2[1],
        "gate": np.stack([np.tile(g, (128, 1)), np.tile(1.0 - g, (128, 1))]).astype(np.float32),
        "offs": striped(slot_token),
        "pos1": striped(pos[0]),
        "pos2": striped(pos[1]),
    }


def reference(x_words, x_scales, w1_words, w1_scales, w3_words, w3_scales, w2_words, w2_scales, gate, offs, pos1, pos2):
    w1 = np.stack([unpack_weight(w1_words[e], w1_scales[e], "e2m1") for e in range(E)])
    w3 = np.stack([unpack_weight(w3_words[e], w3_scales[e], "e2m1") for e in range(E)])
    w2 = unpack_weight(w2_words, w2_scales, "e4m3")
    idx = unstriped(offs)
    xq = unpack_weight(x_words, x_scales, "e4m3")[:, idx]
    h = relu(by_expert(w1, xq)) * by_expert(w3, xq)
    c = sum(f64(gate[r, :1]) * h[:, unstriped(p)] for r, p in enumerate((pos1, pos2)))
    return w2.T @ mxq(c, 0, "e4m3")

@@ -1,0 +1,196 @@
+from contextlib import ExitStack
+
+import concourse.mybir as mybir
+from concourse.masks import make_identity
+
+K, T, E, C, H, N = 512, 512, 8, 128, 512, 128
+FLOPS = 2 * (2 * K * H * E * C + H * N * T)
+
+F32 = mybir.dt.float32
+BF16 = mybir.dt.bfloat16
+I32 = mybir.dt.int32
+U32 = mybir.dt.uint32
+U16 = mybir.dt.uint16
+U8 = mybir.dt.uint8
+FP8X4 = mybir.dt.float8_e4m3fn_x4
+FP4X4 = mybir.dt.float4_e2m1fn_x4
+MULT = mybir.AluOpType.mult
+RELU = mybir.ActivationFunctionType.Relu
+
+P = 128
+SLOTS = E * C
+GROUP = 4
+GROUPS = E // GROUP
+GROUP_SLOTS = GROUP * C
+ROW_TILES = H // P
+BLOCKS = T // P
+LAST_CHUNKS = ((0, 2), (2, 3), (3, 4))
+
+
+def tile_moe_sdn_glu_relu_kernel(
+    tc, x_words, x_scales, w1_words, w1_scales, w3_words, w3_scales, w2_words, w2_scales, gate, offs, pos1, pos2, out
+):
+    nc = tc.nc
+    with ExitStack() as ctx:
+        keep = ctx.enter_context(tc.tile_pool(name="keep", bufs=1))
+        psum = ctx.enter_context(tc.psum_pool(name="psum", bufs=2))
+
+        def sb(name, shape, dtype):
+            return keep.tile(shape, dtype, name=name, align_bytes=64)
+
+        def bank(tag, bufs):
+            return psum.tile([P, 512], F32, name=tag, tag=tag, bufs=bufs)
+
+        offs_sb = keep.tile([P, SLOTS // 16], U16, name="offs_sb")
+        pos_sb = [keep.tile([P, T // 16], U16, name="pos%d_sb" % r) for r in range(2)]
+        xw = sb("xw", [P, 2 * T], I32)
+        xs = sb("xs", [P, 2 * T], U8)
+        ws = [sb("ws%d" % m, [P, E, H], U8) for m in range(2)]
+        w2s = sb("w2s", [P, N], U8)
+        w2w = sb("w2w", [P, 4 * N], U8)
+        gate_sb = sb("gate_sb", [P, 2, T], F32)
+        ident = sb("ident", [P, P], F32)
+        warm = sb("warm", [P, 16], F32)
+
+        nc.vector.memset(xs[:].bitcast(I32), 0)
+        nc.vector.memset(xw[:, T:], 0)
+        nc.vector.memset(ws[0][:].bitcast(I32), 0)
+        nc.vector.memset(ws[1][:].bitcast(I32), 0)
+        nc.vector.memset(w2s[:].bitcast(I32), 0)
+        nc.gpsimd.memset(warm[:, 0:8], 0.0)
+        nc.scalar.activation(warm[:, 8:16], warm[:, 0:8], RELU)
+        make_identity(nc, ident[:])
+
+        def load_scales(plane, rows):
+            for r in range(4):
+                nc.sync.dma_start(plane[r:P:32], rows[r:16:4])
+
+        w_words = [w.rearrange("e s p n -> p (e s) n").bitcast(I32) for w in (w1_words, w3_words)]
+        w_scales = [w.rearrange("e s b n -> b (e s) n").bitcast(I32) for w in (w1_scales, w3_scales)]
+        early = [[sb("we%d%d" % (m, g), [P, GROUP, 512], U8) for g in range(GROUPS)] for m in range(2)]
+        late = [sb("wl%d" % m, [P, E, 512], U8) for m in range(2)]
+
+        nc.sync.dma_start(offs_sb[:], offs)
+        nc.sync.dma_start(xw[:, :T], x_words[0].rearrange("p t d -> p (t d)").bitcast(I32))
+        load_scales(xs[:, :T].bitcast(I32), x_scales[0].bitcast(I32))
+        for m in range(2):
+            nc.sync.dma_start(early[m][0][:].bitcast(I32), w_words[m][:, 0:GROUP, 0:128])
+        for m in range(2):
+            load_scales(ws[m][:].bitcast(I32), w_scales[m])
+        for m in range(2):
+            nc.sync.dma_start(early[m][1][:].bitcast(I32), w_words[m][:, GROUP:E, 0:128])
+        nc.sync.dma_start(pos_sb[0][:], pos1)
+        nc.sync.dma_start(pos_sb[1][:], pos2)
+        nc.sync.dma_start(gate_sb[:], gate.rearrange("r p t -> p r t"))
+        for m in range(2):
+            nc.sync.dma_start(late[m][:].bitcast(I32), w_words[m][:, :, 128:256])
+        nc.sync.dma_start(w2w[:].bitcast(I32), w2_words[0].rearrange("p n d -> p (n d)").bitcast(I32))
+        load_scales(w2s[:].bitcast(I32), w2_scales[0].bitcast(I32))
+
+        xg = [sb("xg%d" % g, [P, GROUP_SLOTS], U32) for g in range(GROUPS)]
+        sg = [sb("sg%d" % g, [P, GROUP_SLOTS], U8) for g in range(GROUPS)]
+        for g in range(GROUPS):
+            cols = offs_sb[:, g * GROUP_SLOTS // 16 : (g + 1) * GROUP_SLOTS // 16]
+            nc.vector.tensor_copy(xg[g][:], xw[:].bitcast(U32).indirect(cols))
+            nc.vector.tensor_copy(sg[g][:], xs[:].indirect(cols))
+
+        h = [sb("h%d" % j, [P, SLOTS], F32) for j in range(ROW_TILES)]
+        c_rows = sb("c_rows", [P, BLOCKS, 2, P, 2], BF16)
+
+        def hidden(g, j):
+            sums = [bank("a", 2), bank("b", 2)]
+            for m in range(2):
+                for el in range(GROUP):
+                    e = g * GROUP + el
+                    if j < 2:
+                        words = early[m][g][:, el, 256 * j : 256 * (j + 1)]
+                    else:
+                        words = late[m][:, e, 256 * (j - 2) : 256 * (j - 1)]
+                    slots = slice(el * C, (el + 1) * C)
+                    nc.tensor.matmul_mx(
+                        out=sums[m][:, slots],
+                        lhsT=words.bitcast(FP4X4),
+                        lhsT_scale=ws[m][:, e, P * j : P * (j + 1)],
+                        rhs=xg[g][:, slots].bitcast(FP8X4),
+                        rhs_scale=sg[g][:, slots],
+                        start=True,
+                        stop=True,
+                    )
+            gated = sb("gated%d%d" % (g, j), [P, GROUP_SLOTS], F32)
+            nc.scalar.activation(gated[:], sums[0][:], RELU)
+            nc.vector.tensor_tensor(h[j][:, g * GROUP_SLOTS : (g + 1) * GROUP_SLOTS], sums[1][:], gated[:], MULT)
+
+        def combine(j, q0, q1):
+            width = (q1 - q0) * P
+            terms = []
+            for r in range(2):
+                term = sb("term%d%d%d" % (j, q0, r), [P, width], F32)
+                nc.vector.tensor_tensor(
+                    term[:],
+                    h[j][:].indirect(pos_sb[r][:, q0 * P // 16 : q1 * P // 16]),
+                    gate_sb[:, r, q0 * P : q1 * P],
+                    MULT,
+                )
+                terms.append(term)
+            total = bank("t", 4)
+            for q in range(q1 - q0):
+                for r in range(2):
+                    nc.tensor.matmul(
+                        total[:, q * P : (q + 1) * P],
+                        lhsT=terms[r][:, q * P : (q + 1) * P],
+                        rhs=ident[:],
+                        is_transpose=True,
+                        start=(r == 0),
+                        stop=(r == 1),
+                    )
+            view = total[:, :width].rearrange("t (q p u e) -> t q u p e", u=2, e=2, p=32)
+            if q1 - q0 == 1:
+                nc.scalar.copy(c_rows[:, q0, :, 32 * j : 32 * (j + 1), :], view[:, 0])
+            else:
+                for u in range(2):
+                    nc.scalar.copy(c_rows[:, q0:q1, u, 32 * j : 32 * (j + 1), :], view[:, :, u])
+
+        def project(q0, q1):
+            width = (q1 - q0) * P
+            turned = bank("b", 2)
+            for q in range(q1 - q0):
+                for u in range(2):
+                    words = c_rows[:, q0 + q, u].rearrange("t p e -> t (p e)").bitcast(F32)
+                    nc.tensor.transpose(turned[:, (2 * q + u) * P : (2 * q + u + 1) * P], words, ident[:])
+            c_cols = sb("c_cols%d" % q0, [P, 4 * width], BF16)
+            nc.scalar.copy(
+                c_cols[:].bitcast(F32).rearrange("p (q t u) -> p q t u", u=2, t=P),
+                turned[:, : 2 * width].rearrange("p (q u t) -> p q t u", u=2, t=P),
+            )
+            codes = sb("codes%d" % q0, [P, width], U32)
+            scales = sb("scales%d" % q0, [P, width], U8)
+            nc.vector.quantize_mx(out=codes[:].bitcast(FP8X4), scales=scales[:], in_=c_cols[:])
+            acc = bank("a", 2)
+            nc.tensor.matmul_mx(
+                out=acc[:, :width],
+                lhsT=w2w[:].bitcast(FP8X4),
+                lhsT_scale=w2s[:],
+                rhs=codes[:].bitcast(FP8X4),
+                rhs_scale=scales[:],
+                start=True,
+                stop=True,
+            )
+            result = sb("result%d" % q0, [P, width], F32)
+            nc.scalar.copy(result[:], acc[:, :width])
+            nc.sync.dma_start(out[:, q0 * P : q1 * P], result[:])
+
+        hidden(0, 0)
+        hidden(0, 1)
+        hidden(1, 0)
+        combine(0, 0, BLOCKS)
+        hidden(1, 1)
+        combine(1, 0, BLOCKS)
+        hidden(0, 2)
+        hidden(1, 2)
+        combine(2, 0, BLOCKS)
+        hidden(0, 3)
+        hidden(1, 3)
+        for q0, q1 in LAST_CHUNKS:
+            combine(3, q0, q1)
+        for q0, q1 in LAST_CHUNKS:
+            project(q0, q1)

@@ -33,36 +33,40 @@ def tile_moe_sdn_glu_relu_kernel(
     nc = tc.nc
     with ExitStack() as ctx:
         keep = ctx.enter_context(tc.tile_pool(name="keep", bufs=1))
-        psum = ctx.enter_context(tc.psum_pool(name="psum", bufs=2))
+        psum = ctx.enter_context(tc.psum_pool(name="psum", bufs=1))
 
         def sb(name, shape, dtype):
             return keep.tile(shape, dtype, name=name, align_bytes=64)
 
-        def bank(tag, bufs):
-            return psum.tile([P, 512], F32, name=tag, tag=tag, bufs=bufs)
+        def bank(b):
+            return psum.tile([P, 512], F32, name="bank%d" % b)
 
         offs_sb = keep.tile([P, SLOTS // 16], U16, name="offs_sb")
         pos_sb = [keep.tile([P, T // 16], U16, name="pos%d_sb" % r) for r in range(2)]
         xw = sb("xw", [P, 2 * T], I32)
         xs = sb("xs", [P, 2 * T], U8)
-        ws = [sb("ws%d" % m, [P, E, H], U8) for m in range(2)]
+        ws = [[sb("ws%d%d" % (m, a), [P, E, H // 2], U8) for a in range(2)] for m in range(2)]
         w2s = sb("w2s", [P, N], U8)
         w2w = sb("w2w", [P, 4 * N], U8)
         gate_sb = sb("gate_sb", [P, 2, T], F32)
         ident = sb("ident", [P, P], F32)
         warm = sb("warm", [P, 16], F32)
+        gate_rows = sb("gate_rows", [P, 2, P], F32)
+        gate_cols = sb("gate_cols", [P, 2, BLOCKS], F32)
 
         nc.vector.memset(xs[:].bitcast(I32), 0)
+        nc.vector.memset(ws[0][0][:].bitcast(I32), 0)
+        nc.gpsimd.memset(ws[1][0][:].bitcast(I32), 0)
         nc.vector.memset(xw[:, T:], 0)
-        nc.vector.memset(ws[0][:].bitcast(I32), 0)
-        nc.vector.memset(ws[1][:].bitcast(I32), 0)
+        for m in range(2):
+            nc.vector.memset(ws[m][1][:].bitcast(I32), 0)
         nc.vector.memset(w2s[:].bitcast(I32), 0)
         nc.gpsimd.memset(warm[:, 0:8], 0.0)
         nc.scalar.activation(warm[:, 8:16], warm[:, 0:8], RELU)
         make_identity(nc, ident[:])
 
-        def load_scales(plane, rows):
-            for r in range(4):
+        def load_scales(plane, rows, which=range(4)):
+            for r in which:
                 nc.sync.dma_start(plane[r:P:32], rows[r:16:4])
 
         w_words = [w.rearrange("e s p n -> p (e s) n").bitcast(I32) for w in (w1_words, w3_words)]
@@ -72,20 +76,33 @@ def tile_moe_sdn_glu_relu_kernel(
 
         nc.sync.dma_start(offs_sb[:], offs)
         nc.sync.dma_start(xw[:, :T], x_words[0].rearrange("p t d -> p (t d)").bitcast(I32))
+        nc.sync.dma_start(gate_rows[:], gate[:, : P // BLOCKS].rearrange("r a (q t) -> (a q) r t", t=P))
         load_scales(xs[:, :T].bitcast(I32), x_scales[0].bitcast(I32))
         for m in range(2):
             nc.sync.dma_start(early[m][0][:].bitcast(I32), w_words[m][:, 0:GROUP, 0:128])
-        for m in range(2):
-            load_scales(ws[m][:].bitcast(I32), w_scales[m])
+        load_scales(ws[0][0][:].bitcast(I32), w_scales[0][:, :, 0:64])
+        load_scales(ws[1][0][:].bitcast(I32), w_scales[1][:, :, 0:64])
         for m in range(2):
             nc.sync.dma_start(early[m][1][:].bitcast(I32), w_words[m][:, GROUP:E, 0:128])
         nc.sync.dma_start(pos_sb[0][:], pos1)
         nc.sync.dma_start(pos_sb[1][:], pos2)
-        nc.sync.dma_start(gate_sb[:], gate.rearrange("r p t -> p r t"))
         for m in range(2):
             nc.sync.dma_start(late[m][:].bitcast(I32), w_words[m][:, :, 128:256])
+        for m in range(2):
+            load_scales(ws[m][1][:].bitcast(I32), w_scales[m][:, :, 64:128])
         nc.sync.dma_start(w2w[:].bitcast(I32), w2_words[0].rearrange("p n d -> p (n d)").bitcast(I32))
         load_scales(w2s[:].bitcast(I32), w2_scales[0].bitcast(I32))
+
+        turned_gate = bank(6)
+        for r in range(2):
+            nc.tensor.transpose(turned_gate[:, r * P : (r + 1) * P], gate_rows[:, r], ident[:])
+        nc.scalar.copy(gate_cols[:], turned_gate[:, : 2 * P].rearrange("t (r x) -> t r x", r=2)[:, :, :BLOCKS])
+        for r in range(2):
+            spread = bank(7 - r)
+            for q in range(BLOCKS):
+                column = gate_cols[:, r, q : q + 1]
+                nc.tensor.transpose(spread[:, q * P : (q + 1) * P], column.to_broadcast([P, P]), ident[:])
+            nc.scalar.copy(gate_sb[:, r, :], spread[:])
 
         xg = [sb("xg%d" % g, [P, GROUP_SLOTS], U32) for g in range(GROUPS)]
         sg = [sb("sg%d" % g, [P, GROUP_SLOTS], U8) for g in range(GROUPS)]
@@ -97,8 +114,8 @@ def tile_moe_sdn_glu_relu_kernel(
         h = [sb("h%d" % j, [P, SLOTS], F32) for j in range(ROW_TILES)]
         c_rows = sb("c_rows", [P, BLOCKS, 2, P, 2], BF16)
 
-        def hidden(g, j):
-            sums = [bank("a", 2), bank("b", 2)]
+        def first_layer(g, j, bank_a, bank_b):
+            sums = [bank(bank_a), bank(bank_b)]
             for m in range(2):
                 for el in range(GROUP):
                     e = g * GROUP + el
@@ -110,7 +127,7 @@ def tile_moe_sdn_glu_relu_kernel(
                     nc.tensor.matmul_mx(
                         out=sums[m][:, slots],
                         lhsT=words.bitcast(FP4X4),
-                        lhsT_scale=ws[m][:, e, P * j : P * (j + 1)],
+                        lhsT_scale=ws[m][j // 2][:, e, P * (j % 2) : P * (j % 2 + 1)],
                         rhs=xg[g][:, slots].bitcast(FP8X4),
                         rhs_scale=sg[g][:, slots],
                         start=True,
@@ -118,13 +135,15 @@ def tile_moe_sdn_glu_relu_kernel(
                     )
             gated = sb("gated%d%d" % (g, j), [P, GROUP_SLOTS], F32)
             nc.scalar.activation(gated[:], sums[0][:], RELU)
-            nc.vector.tensor_tensor(h[j][:, g * GROUP_SLOTS : (g + 1) * GROUP_SLOTS], sums[1][:], gated[:], MULT)
+            return gated, sums[1]
 
-        def combine(j, q0, q1):
-            width = (q1 - q0) * P
+        def product(g, j, gated, linear):
+            nc.vector.tensor_tensor(h[j][:, g * GROUP_SLOTS : (g + 1) * GROUP_SLOTS], linear[:], gated[:], MULT)
+
+        def fetch(j, q0, q1):
             terms = []
             for r in range(2):
-                term = sb("term%d%d%d" % (j, q0, r), [P, width], F32)
+                term = sb("term%d%d%d" % (j, q0, r), [P, (q1 - q0) * P], F32)
                 nc.vector.tensor_tensor(
                     term[:],
                     h[j][:].indirect(pos_sb[r][:, q0 * P // 16 : q1 * P // 16]),
@@ -132,7 +151,10 @@ def tile_moe_sdn_glu_relu_kernel(
                     MULT,
                 )
                 terms.append(term)
-            total = bank("t", 4)
+            return terms
+
+        def add_up(terms, j, q0, q1, b, copy):
+            total = bank(b)
             for q in range(q1 - q0):
                 for r in range(2):
                     nc.tensor.matmul(
@@ -143,16 +165,16 @@ def tile_moe_sdn_glu_relu_kernel(
                         start=(r == 0),
                         stop=(r == 1),
                     )
-            view = total[:, :width].rearrange("t (q p u e) -> t q u p e", u=2, e=2, p=32)
+            view = total[:, : (q1 - q0) * P].rearrange("t (q p u e) -> t q u p e", u=2, e=2, p=32)
             if q1 - q0 == 1:
-                nc.scalar.copy(c_rows[:, q0, :, 32 * j : 32 * (j + 1), :], view[:, 0])
+                copy(c_rows[:, q0, :, 32 * j : 32 * (j + 1), :], view[:, 0])
             else:
                 for u in range(2):
-                    nc.scalar.copy(c_rows[:, q0:q1, u, 32 * j : 32 * (j + 1), :], view[:, :, u])
+                    copy(c_rows[:, q0:q1, u, 32 * j : 32 * (j + 1), :], view[:, :, u])
 
-        def project(q0, q1):
+        def project(q0, q1, bank_turned, bank_acc, copy_out):
             width = (q1 - q0) * P
-            turned = bank("b", 2)
+            turned = bank(bank_turned)
             for q in range(q1 - q0):
                 for u in range(2):
                     words = c_rows[:, q0 + q, u].rearrange("t p e -> t (p e)").bitcast(F32)
@@ -165,7 +187,7 @@ def tile_moe_sdn_glu_relu_kernel(
             codes = sb("codes%d" % q0, [P, width], U32)
             scales = sb("scales%d" % q0, [P, width], U8)
             nc.vector.quantize_mx(out=codes[:].bitcast(FP8X4), scales=scales[:], in_=c_cols[:])
-            acc = bank("a", 2)
+            acc = bank(bank_acc)
             nc.tensor.matmul_mx(
                 out=acc[:, :width],
                 lhsT=w2w[:].bitcast(FP8X4),
@@ -176,21 +198,42 @@ def tile_moe_sdn_glu_relu_kernel(
                 stop=True,
             )
             result = sb("result%d" % q0, [P, width], F32)
-            nc.scalar.copy(result[:], acc[:, :width])
+            copy_out(result[:], acc[:, :width])
             nc.sync.dma_start(out[:, q0 * P : q1 * P], result[:])
 
-        hidden(0, 0)
-        hidden(0, 1)
-        hidden(1, 0)
-        combine(0, 0, BLOCKS)
-        hidden(1, 1)
-        combine(1, 0, BLOCKS)
-        hidden(0, 2)
-        hidden(1, 2)
-        combine(2, 0, BLOCKS)
-        hidden(0, 3)
-        hidden(1, 3)
-        for q0, q1 in LAST_CHUNKS:
-            combine(3, q0, q1)
-        for q0, q1 in LAST_CHUNKS:
-            project(q0, q1)
+        units = [(0, 0), (0, 1), (1, 0), (1, 1), (0, 2), (1, 2), (0, 3), (1, 3)]
+        sums = {}
+
+        def start_unit(k):
+            sums[k] = first_layer(*units[k], k % 2, 2 + k % 4)
+
+        def end_unit(k):
+            product(*units[k], *sums[k])
+
+        for k in range(4):
+            start_unit(k)
+        for k in range(3):
+            end_unit(k)
+            start_unit(k + 4)
+        terms0 = fetch(0, 0, BLOCKS)
+        end_unit(3)
+        start_unit(7)
+        terms1 = fetch(1, 0, BLOCKS)
+        end_unit(4)
+        end_unit(5)
+        terms2 = fetch(2, 0, 2)
+        end_unit(6)
+        end_unit(7)
+        add_up(terms0, 0, 0, BLOCKS, 0, nc.scalar.copy)
+        add_up(terms1, 1, 0, BLOCKS, 1, nc.scalar.copy)
+        on_scalar, on_vector = nc.scalar.copy, nc.vector.tensor_copy
+        add_up(terms2, 2, 0, 2, 6, on_scalar)
+        add_up(fetch(3, 0, 2), 3, 0, 2, 7, on_scalar)
+        add_up(fetch(2, 2, 3), 2, 2, 3, 2, on_scalar)
+        add_up(fetch(3, 2, 3), 3, 2, 3, 3, on_scalar)
+        add_up(fetch(2, 3, 4), 2, 3, 4, 4, on_scalar)
+        last = fetch(3, 3, 4)
+        project(0, 2, 0, 1, on_scalar)
+        add_up(last, 3, 3, 4, 5, on_vector)
+        project(2, 3, 6, 7, on_scalar)
+        project(3, 4, 2, 3, on_vector)

@@ -33,6 +33,7 @@ def tile_moe_sdn_glu_relu_kernel(
     nc = tc.nc
     with ExitStack() as ctx:
         keep = ctx.enter_context(tc.tile_pool(name="keep", bufs=1))
+        hidden = ctx.enter_context(tc.tile_pool(name="hidden", bufs=1))
         psum = ctx.enter_context(tc.psum_pool(name="psum", bufs=1))
 
         def sb(name, shape, dtype):
@@ -72,10 +73,10 @@ def tile_moe_sdn_glu_relu_kernel(
         w_words = [w.rearrange("e s p n -> p (e s) n").bitcast(I32) for w in (w1_words, w3_words)]
         w_scales = [w.rearrange("e s b n -> b (e s) n").bitcast(I32) for w in (w1_scales, w3_scales)]
         early = [[sb("we%d%d" % (m, g), [P, GROUP, 512], U8) for g in range(GROUPS)] for m in range(2)]
-        late = [sb("wl%d" % m, [P, E, 512], U8) for m in range(2)]
+        late = [[sb("wl%d%d" % (m, g), [P, GROUP, 512], U8) for g in range(GROUPS)] for m in range(2)]
 
-        nc.sync.dma_start(offs_sb[:], offs)
         nc.sync.dma_start(xw[:, :T], x_words[0].rearrange("p t d -> p (t d)").bitcast(I32))
+        nc.sync.dma_start(offs_sb[:], offs)
         nc.sync.dma_start(gate_rows[:], gate[:, : P // BLOCKS].rearrange("r a (q t) -> (a q) r t", t=P))
         load_scales(xs[:, :T].bitcast(I32), x_scales[0].bitcast(I32))
         for m in range(2):
@@ -87,9 +88,11 @@ def tile_moe_sdn_glu_relu_kernel(
         nc.sync.dma_start(pos_sb[0][:], pos1)
         nc.sync.dma_start(pos_sb[1][:], pos2)
         for m in range(2):
-            nc.sync.dma_start(late[m][:].bitcast(I32), w_words[m][:, :, 128:256])
+            nc.sync.dma_start(late[m][0][:].bitcast(I32), w_words[m][:, 0:GROUP, 128:256])
         for m in range(2):
             load_scales(ws[m][1][:].bitcast(I32), w_scales[m][:, :, 64:128])
+        for m in range(2):
+            nc.sync.dma_start(late[m][1][:].bitcast(I32), w_words[m][:, GROUP:E, 128:256])
         nc.sync.dma_start(w2w[:].bitcast(I32), w2_words[0].rearrange("p n d -> p (n d)").bitcast(I32))
         load_scales(w2s[:].bitcast(I32), w2_scales[0].bitcast(I32))
 
@@ -111,7 +114,7 @@ def tile_moe_sdn_glu_relu_kernel(
             nc.vector.tensor_copy(xg[g][:], xw[:].bitcast(U32).indirect(cols))
             nc.vector.tensor_copy(sg[g][:], xs[:].indirect(cols))
 
-        h = [sb("h%d" % j, [P, SLOTS], F32) for j in range(ROW_TILES)]
+        h = [hidden.tile([P, SLOTS], F32, name="h%d" % j, offset=at) for j, at in enumerate((8192, 2048, 0, 4096))]
         c_rows = sb("c_rows", [P, BLOCKS, 2, P, 2], BF16)
 
         def first_layer(g, j, bank_a, bank_b):
@@ -122,7 +125,7 @@ def tile_moe_sdn_glu_relu_kernel(
                     if j < 2:
                         words = early[m][g][:, el, 256 * j : 256 * (j + 1)]
                     else:
-                        words = late[m][:, e, 256 * (j - 2) : 256 * (j - 1)]
+                        words = late[m][g][:, el, 256 * (j - 2) : 256 * (j - 1)]
                     slots = slice(el * C, (el + 1) * C)
                     nc.tensor.matmul_mx(
                         out=sums[m][:, slots],
@@ -137,8 +140,12 @@ def tile_moe_sdn_glu_relu_kernel(
             nc.scalar.activation(gated[:], sums[0][:], RELU)
             return gated, sums[1]
 
-        def product(g, j, gated, linear):
-            nc.vector.tensor_tensor(h[j][:, g * GROUP_SLOTS : (g + 1) * GROUP_SLOTS], linear[:], gated[:], MULT)
+        def product(g, j, gated, linear, on_gpsimd=False):
+            if on_gpsimd:
+                copied = sb("copied", [P, GROUP_SLOTS], F32)
+                nc.scalar.copy(copied[:], linear[:])
+                linear = copied
+            (nc.gpsimd if on_gpsimd else nc.vector).tensor_tensor(h[j][:, g * GROUP_SLOTS : (g + 1) * GROUP_SLOTS], linear[:], gated[:], MULT)
 
         def fetch(j, q0, q1):
             terms = []
@@ -201,7 +208,7 @@ def tile_moe_sdn_glu_relu_kernel(
             copy_out(result[:], acc[:, :width])
             nc.sync.dma_start(out[:, q0 * P : q1 * P], result[:])
 
-        units = [(0, 0), (0, 1), (1, 0), (1, 1), (0, 2), (1, 2), (0, 3), (1, 3)]
+        units = [(0, 0), (0, 1), (1, 0), (1, 1), (0, 2), (0, 3), (1, 2), (1, 3)]
         sums = {}
 
         def start_unit(k):
@@ -219,11 +226,11 @@ def tile_moe_sdn_glu_relu_kernel(
         end_unit(3)
         start_unit(7)
         terms1 = fetch(1, 0, BLOCKS)
+        product(*units[5], *sums[5], True)
         end_unit(4)
-        end_unit(5)
-        terms2 = fetch(2, 0, 2)
         end_unit(6)
         end_unit(7)
+        terms2 = fetch(2, 0, 2)
         add_up(terms0, 0, 0, BLOCKS, 0, nc.scalar.copy)
         add_up(terms1, 1, 0, BLOCKS, 1, nc.scalar.copy)
         on_scalar, on_vector = nc.scalar.copy, nc.vector.tensor_copy

@@ -45,7 +45,7 @@ def tile_moe_sdn_glu_relu_kernel(
         offs_sb = keep.tile([P, SLOTS // 16], U16, name="offs_sb")
         pos_sb = [keep.tile([P, T // 16], U16, name="pos%d_sb" % r) for r in range(2)]
         xw = sb("xw", [P, 2 * T], I32)
-        xs = sb("xs", [P, 2 * T], U8)
+        xs = sb("xs", [P, T], U8)
         ws = [[sb("ws%d%d" % (m, a), [P, E, H // 2], U8) for a in range(2)] for m in range(2)]
         w2s = sb("w2s", [P, N], U8)
         w2w = sb("w2w", [P, 4 * N], U8)
@@ -112,7 +112,9 @@ def tile_moe_sdn_glu_relu_kernel(
         for g in range(GROUPS):
             cols = offs_sb[:, g * GROUP_SLOTS // 16 : (g + 1) * GROUP_SLOTS // 16]
             nc.vector.tensor_copy(xg[g][:], xw[:].bitcast(U32).indirect(cols))
-            nc.vector.tensor_copy(sg[g][:], xs[:].indirect(cols))
+            for half in range(2):
+                part = offs_sb[:, (2 * g + half) * 16 : (2 * g + half + 1) * 16]
+                nc.vector.tensor_copy(sg[g][:, 256 * half : 256 * (half + 1)], xs[:].indirect(part))
 
         h = [hidden.tile([P, SLOTS], F32, name="h%d" % j, offset=at) for j, at in enumerate((8192, 2048, 0, 4096))]
         c_rows = sb("c_rows", [P, BLOCKS, 2, P, 2], BF16)
@@ -219,12 +221,10 @@ def tile_moe_sdn_glu_relu_kernel(
 
         for k in range(4):
             start_unit(k)
-        for k in range(3):
+        for k in range(4):
             end_unit(k)
             start_unit(k + 4)
         terms0 = fetch(0, 0, BLOCKS)
-        end_unit(3)
-        start_unit(7)
         terms1 = fetch(1, 0, BLOCKS)
         product(*units[5], *sums[5], True)
         end_unit(4)

@@ -16,6 +16,7 @@ FP8X4 = mybir.dt.float8_e4m3fn_x4
 FP4X4 = mybir.dt.float4_e2m1fn_x4
 MULT = mybir.AluOpType.mult
 RELU = mybir.ActivationFunctionType.Relu
+COPY = mybir.ActivationFunctionType.Copy
 
 P = 128
 SLOTS = E * C
@@ -34,6 +35,7 @@ def tile_moe_sdn_glu_relu_kernel(
     with ExitStack() as ctx:
         keep = ctx.enter_context(tc.tile_pool(name="keep", bufs=1))
         hidden = ctx.enter_context(tc.tile_pool(name="hidden", bufs=1))
+        shared = ctx.enter_context(tc.tile_pool(name="shared", bufs=1))
         psum = ctx.enter_context(tc.psum_pool(name="psum", bufs=1))
 
         def sb(name, shape, dtype):
@@ -44,49 +46,44 @@ def tile_moe_sdn_glu_relu_kernel(
 
         offs_sb = keep.tile([P, SLOTS // 16], U16, name="offs_sb")
         pos_sb = [keep.tile([P, T // 16], U16, name="pos%d_sb" % r) for r in range(2)]
-        xw = sb("xw", [P, 2 * T], I32)
-        xs = sb("xs", [P, T], U8)
+        xw = sb("xw", [P, T], I32)
+        xs = shared.tile([P, T], U8, name="xs", align_bytes=64, offset=0)
         ws = [[sb("ws%d%d" % (m, a), [P, E, H // 2], U8) for a in range(2)] for m in range(2)]
         w2s = sb("w2s", [P, N], U8)
         w2w = sb("w2w", [P, 4 * N], U8)
-        gate_sb = sb("gate_sb", [P, 2, T], F32)
+        gate_sb = [sb("gate%d_sb" % r, [P, T], F32) for r in range(2)]
         ident = sb("ident", [P, P], F32)
-        warm = sb("warm", [P, 16], F32)
-        gate_rows = sb("gate_rows", [P, 2, P], F32)
-        gate_cols = sb("gate_cols", [P, 2, BLOCKS], F32)
 
         nc.vector.memset(xs[:].bitcast(I32), 0)
         nc.vector.memset(ws[0][0][:].bitcast(I32), 0)
         nc.gpsimd.memset(ws[1][0][:].bitcast(I32), 0)
-        nc.vector.memset(xw[:, T:], 0)
         for m in range(2):
             nc.vector.memset(ws[m][1][:].bitcast(I32), 0)
         nc.vector.memset(w2s[:].bitcast(I32), 0)
-        nc.gpsimd.memset(warm[:, 0:8], 0.0)
-        nc.scalar.activation(warm[:, 8:16], warm[:, 0:8], RELU)
-        make_identity(nc, ident[:])
 
-        def load_scales(plane, rows, which=range(4)):
+        def load_scales(plane, rows, which=range(4), queue=nc.sync):
             for r in which:
-                nc.sync.dma_start(plane[r:P:32], rows[r:16:4])
+                queue.dma_start(plane[r:P:32], rows[r:16:4])
 
         w_words = [w.rearrange("e s p n -> p (e s) n").bitcast(I32) for w in (w1_words, w3_words)]
         w_scales = [w.rearrange("e s b n -> b (e s) n").bitcast(I32) for w in (w1_scales, w3_scales)]
         early = [[sb("we%d%d" % (m, g), [P, GROUP, 512], U8) for g in range(GROUPS)] for m in range(2)]
         late = [[sb("wl%d%d" % (m, g), [P, GROUP, 512], U8) for g in range(GROUPS)] for m in range(2)]
 
-        nc.sync.dma_start(xw[:, :T], x_words[0].rearrange("p t d -> p (t d)").bitcast(I32))
+        nc.sync.dma_start(xw[:], x_words[0].rearrange("p t d -> p (t d)").bitcast(I32))
         nc.sync.dma_start(offs_sb[:], offs)
-        nc.sync.dma_start(gate_rows[:], gate[:, : P // BLOCKS].rearrange("r a (q t) -> (a q) r t", t=P))
         load_scales(xs[:, :T].bitcast(I32), x_scales[0].bitcast(I32))
         for m in range(2):
             nc.sync.dma_start(early[m][0][:].bitcast(I32), w_words[m][:, 0:GROUP, 0:128])
+        load_scales(ws[1][0][:].bitcast(I32), w_scales[1][:, :, 0:64], range(2, 4), nc.gpsimd)
         load_scales(ws[0][0][:].bitcast(I32), w_scales[0][:, :, 0:64])
-        load_scales(ws[1][0][:].bitcast(I32), w_scales[1][:, :, 0:64])
+        load_scales(ws[1][0][:].bitcast(I32), w_scales[1][:, :, 0:64], range(2))
         for m in range(2):
             nc.sync.dma_start(early[m][1][:].bitcast(I32), w_words[m][:, GROUP:E, 0:128])
-        nc.sync.dma_start(pos_sb[0][:], pos1)
-        nc.sync.dma_start(pos_sb[1][:], pos2)
+        for r, pos in enumerate((pos1, pos2)):
+            nc.sync.dma_start(pos_sb[r][:], pos)
+            nc.sync.dma_start(gate_sb[r][:], gate[r])
+        make_identity(nc, ident[:])
         for m in range(2):
             nc.sync.dma_start(late[m][0][:].bitcast(I32), w_words[m][:, 0:GROUP, 128:256])
         for m in range(2):
@@ -96,58 +93,49 @@ def tile_moe_sdn_glu_relu_kernel(
         nc.sync.dma_start(w2w[:].bitcast(I32), w2_words[0].rearrange("p n d -> p (n d)").bitcast(I32))
         load_scales(w2s[:].bitcast(I32), w2_scales[0].bitcast(I32))
 
-        turned_gate = bank(6)
-        for r in range(2):
-            nc.tensor.transpose(turned_gate[:, r * P : (r + 1) * P], gate_rows[:, r], ident[:])
-        nc.scalar.copy(gate_cols[:], turned_gate[:, : 2 * P].rearrange("t (r x) -> t r x", r=2)[:, :, :BLOCKS])
-        for r in range(2):
-            spread = bank(7 - r)
-            for q in range(BLOCKS):
-                column = gate_cols[:, r, q : q + 1]
-                nc.tensor.transpose(spread[:, q * P : (q + 1) * P], column.to_broadcast([P, P]), ident[:])
-            nc.scalar.copy(gate_sb[:, r, :], spread[:])
-
-        xg = [sb("xg%d" % g, [P, GROUP_SLOTS], U32) for g in range(GROUPS)]
+        xg = [sb("xg0", [P, GROUP_SLOTS], U32), shared.tile([P, GROUP_SLOTS], U32, name="xg1", align_bytes=64, offset=0)]
         sg = [sb("sg%d" % g, [P, GROUP_SLOTS], U8) for g in range(GROUPS)]
-        for g in range(GROUPS):
-            cols = offs_sb[:, g * GROUP_SLOTS // 16 : (g + 1) * GROUP_SLOTS // 16]
-            nc.vector.tensor_copy(xg[g][:], xw[:].bitcast(U32).indirect(cols))
+        xs_moved = sb("xs_moved", [P, T], U8)
+        nc.vector.tensor_copy(xs_moved[:].bitcast(I32), xs[:].bitcast(I32))
+        for g, window in enumerate((xs, xs_moved)):
             for half in range(2):
                 part = offs_sb[:, (2 * g + half) * 16 : (2 * g + half + 1) * 16]
-                nc.vector.tensor_copy(sg[g][:, 256 * half : 256 * (half + 1)], xs[:].indirect(part))
+                nc.vector.tensor_copy(xg[g][:, 256 * half : 256 * (half + 1)], xw[:].bitcast(U32).indirect(part))
+                nc.vector.tensor_copy(sg[g][:, 256 * half : 256 * (half + 1)], window[:].indirect(part))
 
         h = [hidden.tile([P, SLOTS], F32, name="h%d" % j, offset=at) for j, at in enumerate((8192, 2048, 0, 4096))]
         c_rows = sb("c_rows", [P, BLOCKS, 2, P, 2], BF16)
 
-        def first_layer(g, j, bank_a, bank_b):
-            sums = [bank(bank_a), bank(bank_b)]
-            for m in range(2):
-                for el in range(GROUP):
-                    e = g * GROUP + el
-                    if j < 2:
-                        words = early[m][g][:, el, 256 * j : 256 * (j + 1)]
-                    else:
-                        words = late[m][g][:, el, 256 * (j - 2) : 256 * (j - 1)]
-                    slots = slice(el * C, (el + 1) * C)
-                    nc.tensor.matmul_mx(
-                        out=sums[m][:, slots],
-                        lhsT=words.bitcast(FP4X4),
-                        lhsT_scale=ws[m][j // 2][:, e, P * (j % 2) : P * (j % 2 + 1)],
-                        rhs=xg[g][:, slots].bitcast(FP8X4),
-                        rhs_scale=sg[g][:, slots],
-                        start=True,
-                        stop=True,
-                    )
-            gated = sb("gated%d%d" % (g, j), [P, GROUP_SLOTS], F32)
-            nc.scalar.activation(gated[:], sums[0][:], RELU)
-            return gated, sums[1]
+        def passes(m, j, experts, b):
+            sums = bank(b)
+            for at, e in enumerate(experts):
+                g, el = divmod(e, GROUP)
+                words = (early, late)[j // 2][m][g][:, el, 256 * (j % 2) : 256 * (j % 2 + 1)]
+                slots = slice(el * C, (el + 1) * C)
+                nc.tensor.matmul_mx(
+                    out=sums[:, at * C : (at + 1) * C],
+                    lhsT=words.bitcast(FP4X4),
+                    lhsT_scale=ws[m][j // 2][:, e, P * (j % 2) : P * (j % 2 + 1)],
+                    rhs=xg[g][:, slots].bitcast(FP8X4),
+                    rhs_scale=sg[g][:, slots],
+                    start=True,
+                    stop=True,
+                )
+            return sums[:, : len(experts) * C]
 
-        def product(g, j, gated, linear, on_gpsimd=False):
+        def leave(sums, name, func):
+            kept = sb(name, [P, sums.shape[1]], F32)
+            nc.scalar.activation(kept[:], sums, func)
+            return kept[:]
+
+        def unit(j, experts, bank_a, bank_b, on_gpsimd=False):
+            name = "%d_%d" % (j, experts[0])
+            gated = leave(passes(0, j, experts, bank_a), "gated" + name, RELU)
+            linear = passes(1, j, experts, bank_b)
             if on_gpsimd:
-                copied = sb("copied", [P, GROUP_SLOTS], F32)
-                nc.scalar.copy(copied[:], linear[:])
-                linear = copied
-            (nc.gpsimd if on_gpsimd else nc.vector).tensor_tensor(h[j][:, g * GROUP_SLOTS : (g + 1) * GROUP_SLOTS], linear[:], gated[:], MULT)
+                linear = leave(linear, "linear" + name, COPY)
+            engine = nc.gpsimd if on_gpsimd else nc.vector
+            return lambda: engine.tensor_tensor(h[j][:, experts[0] * C : (experts[-1] + 1) * C], linear, gated, MULT)
 
         def fetch(j, q0, q1):
             terms = []
@@ -156,7 +144,7 @@ def tile_moe_sdn_glu_relu_kernel(
                 nc.vector.tensor_tensor(
                     term[:],
                     h[j][:].indirect(pos_sb[r][:, q0 * P // 16 : q1 * P // 16]),
-                    gate_sb[:, r, q0 * P : q1 * P],
+                    gate_sb[r][:, q0 * P : q1 * P],
                     MULT,
                 )
                 terms.append(term)
@@ -210,37 +198,30 @@ def tile_moe_sdn_glu_relu_kernel(
             copy_out(result[:], acc[:, :width])
             nc.sync.dma_start(out[:, q0 * P : q1 * P], result[:])
 
-        units = [(0, 0), (0, 1), (1, 0), (1, 1), (0, 2), (0, 3), (1, 2), (1, 3)]
-        sums = {}
-
-        def start_unit(k):
-            sums[k] = first_layer(*units[k], k % 2, 2 + k % 4)
-
-        def end_unit(k):
-            product(*units[k], *sums[k])
-
-        for k in range(4):
-            start_unit(k)
-        for k in range(4):
-            end_unit(k)
-            start_unit(k + 4)
+        low, high = range(0, GROUP), range(GROUP, E)
+        unit(0, low, 0, 2, True)()
+        unit(1, low, 1, 3)()
+        unit(0, high[:2], 4, 5)()
+        unit(1, high[:2], 0, 2)()
+        unit(0, high[2:], 6, 7)()
+        second = unit(1, high[2:], 1, 3)
         terms0 = fetch(0, 0, BLOCKS)
+        second()
+        later = [unit(2, low, 4, 5), unit(3, low, 0, 2, True), unit(2, high, 6, 7), unit(3, high, 1, 3)]
         terms1 = fetch(1, 0, BLOCKS)
-        product(*units[5], *sums[5], True)
-        end_unit(4)
-        end_unit(6)
-        end_unit(7)
+        for product in later:
+            product()
         terms2 = fetch(2, 0, 2)
-        add_up(terms0, 0, 0, BLOCKS, 0, nc.scalar.copy)
-        add_up(terms1, 1, 0, BLOCKS, 1, nc.scalar.copy)
         on_scalar, on_vector = nc.scalar.copy, nc.vector.tensor_copy
-        add_up(terms2, 2, 0, 2, 6, on_scalar)
-        add_up(fetch(3, 0, 2), 3, 0, 2, 7, on_scalar)
+        add_up(terms0, 0, 0, BLOCKS, 1, on_scalar)
+        add_up(terms1, 1, 0, BLOCKS, 6, on_scalar)
+        add_up(terms2, 2, 0, 2, 0, on_scalar)
+        add_up(fetch(3, 0, 2), 3, 0, 2, 4, on_scalar)
         add_up(fetch(2, 2, 3), 2, 2, 3, 2, on_scalar)
-        add_up(fetch(3, 2, 3), 3, 2, 3, 3, on_scalar)
-        add_up(fetch(2, 3, 4), 2, 3, 4, 4, on_scalar)
+        add_up(fetch(3, 2, 3), 3, 2, 3, 5, on_scalar)
+        add_up(fetch(2, 3, 4), 2, 3, 4, 7, on_scalar)
         last = fetch(3, 3, 4)
-        project(0, 2, 0, 1, on_scalar)
-        add_up(last, 3, 3, 4, 5, on_vector)
-        project(2, 3, 6, 7, on_scalar)
-        project(3, 4, 2, 3, on_vector)
+        project(0, 2, 1, 6, on_scalar)
+        add_up(last, 3, 3, 4, 3, on_vector)
+        project(2, 3, 0, 4, on_scalar)
+        project(3, 4, 2, 5, on_vector)

@@ -48,22 +48,24 @@ def tile_moe_sdn_glu_relu_kernel(
         pos_sb = [keep.tile([P, T // 16], U16, name="pos%d_sb" % r) for r in range(2)]
         xw = sb("xw", [P, T], I32)
         xs = shared.tile([P, T], U8, name="xs", align_bytes=64, offset=0)
-        ws = [[sb("ws%d%d" % (m, a), [P, E, H // 2], U8) for a in range(2)] for m in range(2)]
+        ws = [sb("ws%d" % m, [P, E, H], U8) for m in range(2)]
         w2s = sb("w2s", [P, N], U8)
         w2w = sb("w2w", [P, 4 * N], U8)
         gate_sb = [sb("gate%d_sb" % r, [P, T], F32) for r in range(2)]
+        gate_cols = sb("gate_cols", [P, 2, BLOCKS], F32)
         ident = sb("ident", [P, P], F32)
 
         nc.vector.memset(xs[:].bitcast(I32), 0)
-        nc.vector.memset(ws[0][0][:].bitcast(I32), 0)
-        nc.gpsimd.memset(ws[1][0][:].bitcast(I32), 0)
         for m in range(2):
-            nc.vector.memset(ws[m][1][:].bitcast(I32), 0)
+            nc.vector.memset(ws[m][:, :GROUP].bitcast(I32), 0)
+            nc.gpsimd.memset(ws[m][:, GROUP:].bitcast(I32), 0)
+        nc.gpsimd.dma_start(gate_cols[:], gate[:, 0].rearrange("r (p q) -> p r q", q=BLOCKS))
+        make_identity(nc, ident[:])
         nc.vector.memset(w2s[:].bitcast(I32), 0)
 
-        def load_scales(plane, rows, which=range(4), queue=nc.sync):
-            for r in which:
-                queue.dma_start(plane[r:P:32], rows[r:16:4])
+        def load_scales(plane, rows):
+            for r in range(4):
+                nc.sync.dma_start(plane[r:P:32], rows[r:16:4])
 
         w_words = [w.rearrange("e s p n -> p (e s) n").bitcast(I32) for w in (w1_words, w3_words)]
         w_scales = [w.rearrange("e s b n -> b (e s) n").bitcast(I32) for w in (w1_scales, w3_scales)]
@@ -75,23 +77,25 @@ def tile_moe_sdn_glu_relu_kernel(
         load_scales(xs[:, :T].bitcast(I32), x_scales[0].bitcast(I32))
         for m in range(2):
             nc.sync.dma_start(early[m][0][:].bitcast(I32), w_words[m][:, 0:GROUP, 0:128])
-        load_scales(ws[1][0][:].bitcast(I32), w_scales[1][:, :, 0:64], range(2, 4), nc.gpsimd)
-        load_scales(ws[0][0][:].bitcast(I32), w_scales[0][:, :, 0:64])
-        load_scales(ws[1][0][:].bitcast(I32), w_scales[1][:, :, 0:64], range(2))
+            load_scales(ws[m][:].bitcast(I32), w_scales[m])
         for m in range(2):
             nc.sync.dma_start(early[m][1][:].bitcast(I32), w_words[m][:, GROUP:E, 0:128])
-        for r, pos in enumerate((pos1, pos2)):
-            nc.sync.dma_start(pos_sb[r][:], pos)
-            nc.sync.dma_start(gate_sb[r][:], gate[r])
-        make_identity(nc, ident[:])
-        for m in range(2):
-            nc.sync.dma_start(late[m][0][:].bitcast(I32), w_words[m][:, 0:GROUP, 128:256])
-        for m in range(2):
-            load_scales(ws[m][1][:].bitcast(I32), w_scales[m][:, :, 64:128])
-        for m in range(2):
-            nc.sync.dma_start(late[m][1][:].bitcast(I32), w_words[m][:, GROUP:E, 128:256])
+        nc.sync.dma_start(pos_sb[0][:], pos1)
+        nc.sync.dma_start(pos_sb[1][:], pos2)
+        for g in range(GROUPS):
+            for m in range(2):
+                nc.sync.dma_start(late[m][g][:].bitcast(I32), w_words[m][:, g * GROUP : (g + 1) * GROUP, 128:256])
         nc.sync.dma_start(w2w[:].bitcast(I32), w2_words[0].rearrange("p n d -> p (n d)").bitcast(I32))
         load_scales(w2s[:].bitcast(I32), w2_scales[0].bitcast(I32))
+
+        for r in range(2):
+            spread = bank(7 - r)
+            for q in range(BLOCKS):
+                column = gate_cols[:, r, q : q + 1]
+                nc.tensor.transpose(spread[:, q * P : (q + 1) * P], column.to_broadcast([P, P]), ident[:])
+            nc.scalar.activation(
+                gate_sb[r][:].rearrange("p (n q) -> p n q", q=BLOCKS), spread[:].rearrange("p (q n) -> p n q", q=BLOCKS), COPY
+            )
 
         xg = [sb("xg0", [P, GROUP_SLOTS], U32), shared.tile([P, GROUP_SLOTS], U32, name="xg1", align_bytes=64, offset=0)]
         sg = [sb("sg%d" % g, [P, GROUP_SLOTS], U8) for g in range(GROUPS)]
@@ -115,7 +119,7 @@ def tile_moe_sdn_glu_relu_kernel(
                 nc.tensor.matmul_mx(
                     out=sums[:, at * C : (at + 1) * C],
                     lhsT=words.bitcast(FP4X4),
-                    lhsT_scale=ws[m][j // 2][:, e, P * (j % 2) : P * (j % 2 + 1)],
+                    lhsT_scale=ws[m][:, e, P * j : P * (j + 1)],
                     rhs=xg[g][:, slots].bitcast(FP8X4),
                     rhs_scale=sg[g][:, slots],
                     start=True,

@@ -48,7 +48,7 @@ def tile_moe_sdn_glu_relu_kernel(
         pos_sb = [keep.tile([P, T // 16], U16, name="pos%d_sb" % r) for r in range(2)]
         xw = sb("xw", [P, T], I32)
         xs = shared.tile([P, T], U8, name="xs", align_bytes=64, offset=0)
-        ws = [sb("ws%d" % m, [P, E, H], U8) for m in range(2)]
+        ws = [[sb("ws%d%d" % (m, a), [P, E, H // 2], U8) for a in range(2)] for m in range(2)]
         w2s = sb("w2s", [P, N], U8)
         w2w = sb("w2w", [P, 4 * N], U8)
         gate_sb = [sb("gate%d_sb" % r, [P, T], F32) for r in range(2)]
@@ -56,11 +56,11 @@ def tile_moe_sdn_glu_relu_kernel(
         ident = sb("ident", [P, P], F32)
 
         nc.vector.memset(xs[:].bitcast(I32), 0)
-        for m in range(2):
-            nc.vector.memset(ws[m][:, :GROUP].bitcast(I32), 0)
-            nc.gpsimd.memset(ws[m][:, GROUP:].bitcast(I32), 0)
-        nc.gpsimd.dma_start(gate_cols[:], gate[:, 0].rearrange("r (p q) -> p r q", q=BLOCKS))
+        nc.vector.memset(ws[0][0][:].bitcast(I32), 0)
+        nc.gpsimd.memset(ws[1][0][:].bitcast(I32), 0)
         make_identity(nc, ident[:])
+        for m in range(2):
+            nc.vector.memset(ws[m][1][:].bitcast(I32), 0)
         nc.vector.memset(w2s[:].bitcast(I32), 0)
 
         def load_scales(plane, rows):
@@ -74,17 +74,21 @@ def tile_moe_sdn_glu_relu_kernel(
 
         nc.sync.dma_start(xw[:], x_words[0].rearrange("p t d -> p (t d)").bitcast(I32))
         nc.sync.dma_start(offs_sb[:], offs)
-        load_scales(xs[:, :T].bitcast(I32), x_scales[0].bitcast(I32))
+        load_scales(xs[:].bitcast(I32), x_scales[0].bitcast(I32))
+        nc.sync.dma_start(gate_cols[:], gate[:, 0].rearrange("r (p q) -> p r q", q=BLOCKS))
         for m in range(2):
             nc.sync.dma_start(early[m][0][:].bitcast(I32), w_words[m][:, 0:GROUP, 0:128])
-            load_scales(ws[m][:].bitcast(I32), w_scales[m])
+            load_scales(ws[m][0][:].bitcast(I32), w_scales[m][:, :, 0:64])
         for m in range(2):
             nc.sync.dma_start(early[m][1][:].bitcast(I32), w_words[m][:, GROUP:E, 0:128])
         nc.sync.dma_start(pos_sb[0][:], pos1)
         nc.sync.dma_start(pos_sb[1][:], pos2)
-        for g in range(GROUPS):
-            for m in range(2):
-                nc.sync.dma_start(late[m][g][:].bitcast(I32), w_words[m][:, g * GROUP : (g + 1) * GROUP, 128:256])
+        for m in range(2):
+            nc.sync.dma_start(late[m][0][:].bitcast(I32), w_words[m][:, 0:GROUP, 128:256])
+        for m in range(2):
+            load_scales(ws[m][1][:].bitcast(I32), w_scales[m][:, :, 64:128])
+        for m in range(2):
+            nc.sync.dma_start(late[m][1][:].bitcast(I32), w_words[m][:, GROUP:E, 128:256])
         nc.sync.dma_start(w2w[:].bitcast(I32), w2_words[0].rearrange("p n d -> p (n d)").bitcast(I32))
         load_scales(w2s[:].bitcast(I32), w2_scales[0].bitcast(I32))
 
@@ -119,7 +123,7 @@ def tile_moe_sdn_glu_relu_kernel(
                 nc.tensor.matmul_mx(
                     out=sums[:, at * C : (at + 1) * C],
                     lhsT=words.bitcast(FP4X4),
-                    lhsT_scale=ws[m][:, e, P * j : P * (j + 1)],
+                    lhsT_scale=ws[m][j // 2][:, e, P * (j % 2) : P * (j % 2 + 1)],
                     rhs=xg[g][:, slots].bitcast(FP8X4),
                     rhs_scale=sg[g][:, slots],
                     start=True,

@@ -25,7 +25,7 @@ GROUPS = E // GROUP
 GROUP_SLOTS = GROUP * C
 ROW_TILES = H // P
 BLOCKS = T // P
-LAST_CHUNKS = ((0, 2), (2, 3), (3, 4))
+EARLY_LOADS = ((0, 4), (4, 6), (6, 8))
 
 
 def tile_moe_sdn_glu_relu_kernel(
@@ -56,31 +56,33 @@ def tile_moe_sdn_glu_relu_kernel(
         ident = sb("ident", [P, P], F32)
 
         nc.vector.memset(xs[:].bitcast(I32), 0)
-        nc.vector.memset(ws[0][0][:].bitcast(I32), 0)
-        nc.gpsimd.memset(ws[1][0][:].bitcast(I32), 0)
+        for m in range(2):
+            nc.vector.memset(ws[m][0][:, :GROUP].bitcast(I32), 0)
+            nc.gpsimd.memset(ws[m][0][:, GROUP:].bitcast(I32), 0)
         make_identity(nc, ident[:])
         for m in range(2):
             nc.vector.memset(ws[m][1][:].bitcast(I32), 0)
         nc.vector.memset(w2s[:].bitcast(I32), 0)
 
-        def load_scales(plane, rows):
-            for r in range(4):
-                nc.sync.dma_start(plane[r:P:32], rows[r:16:4])
+        def load_scales(plane, rows, queues=(nc.sync,) * 4):
+            for r, queue in enumerate(queues):
+                queue.dma_start(plane[r:P:32], rows[r:16:4])
 
         w_words = [w.rearrange("e s p n -> p (e s) n").bitcast(I32) for w in (w1_words, w3_words)]
         w_scales = [w.rearrange("e s b n -> b (e s) n").bitcast(I32) for w in (w1_scales, w3_scales)]
-        early = [[sb("we%d%d" % (m, g), [P, GROUP, 512], U8) for g in range(GROUPS)] for m in range(2)]
+        early = [[sb("we%d%d" % (m, e0), [P, e1 - e0, 512], U8) for e0, e1 in EARLY_LOADS] for m in range(2)]
         late = [[sb("wl%d%d" % (m, g), [P, GROUP, 512], U8) for g in range(GROUPS)] for m in range(2)]
 
         nc.sync.dma_start(xw[:], x_words[0].rearrange("p t d -> p (t d)").bitcast(I32))
         nc.sync.dma_start(offs_sb[:], offs)
-        load_scales(xs[:].bitcast(I32), x_scales[0].bitcast(I32))
+        load_scales(xs[:].bitcast(I32), x_scales[0].bitcast(I32), (nc.sync, nc.scalar) * 2)
         nc.sync.dma_start(gate_cols[:], gate[:, 0].rearrange("r (p q) -> p r q", q=BLOCKS))
         for m in range(2):
             nc.sync.dma_start(early[m][0][:].bitcast(I32), w_words[m][:, 0:GROUP, 0:128])
             load_scales(ws[m][0][:].bitcast(I32), w_scales[m][:, :, 0:64])
-        for m in range(2):
-            nc.sync.dma_start(early[m][1][:].bitcast(I32), w_words[m][:, GROUP:E, 0:128])
+        for at, (e0, e1) in list(enumerate(EARLY_LOADS))[1:]:
+            for m in range(2):
+                nc.sync.dma_start(early[m][at][:].bitcast(I32), w_words[m][:, e0:e1, 0:128])
         nc.sync.dma_start(pos_sb[0][:], pos1)
         nc.sync.dma_start(pos_sb[1][:], pos2)
         for m in range(2):
@@ -118,7 +120,12 @@ def tile_moe_sdn_glu_relu_kernel(
             sums = bank(b)
             for at, e in enumerate(experts):
                 g, el = divmod(e, GROUP)
-                words = (early, late)[j // 2][m][g][:, el, 256 * (j % 2) : 256 * (j % 2 + 1)]
+                if j < 2:
+                    load = max(e // 2 - 1, 0)
+                    row = early[m][load][:, e - EARLY_LOADS[load][0]]
+                else:
+                    row = late[m][g][:, el]
+                words = row[:, 256 * (j % 2) : 256 * (j % 2 + 1)]
                 slots = slice(el * C, (el + 1) * C)
                 nc.tensor.matmul_mx(
                     out=sums[:, at * C : (at + 1) * C],
@@ -145,18 +152,18 @@ def tile_moe_sdn_glu_relu_kernel(
             engine = nc.gpsimd if on_gpsimd else nc.vector
             return lambda: engine.tensor_tensor(h[j][:, experts[0] * C : (experts[-1] + 1) * C], linear, gated, MULT)
 
+        def fetch_one(j, q0, q1, r):
+            term = sb("term%d%d%d" % (j, q0, r), [P, (q1 - q0) * P], F32)
+            nc.vector.tensor_tensor(
+                term[:],
+                h[j][:].indirect(pos_sb[r][:, q0 * P // 16 : q1 * P // 16]),
+                gate_sb[r][:, q0 * P : q1 * P],
+                MULT,
+            )
+            return term
+
         def fetch(j, q0, q1):
-            terms = []
-            for r in range(2):
-                term = sb("term%d%d%d" % (j, q0, r), [P, (q1 - q0) * P], F32)
-                nc.vector.tensor_tensor(
-                    term[:],
-                    h[j][:].indirect(pos_sb[r][:, q0 * P // 16 : q1 * P // 16]),
-                    gate_sb[r][:, q0 * P : q1 * P],
-                    MULT,
-                )
-                terms.append(term)
-            return terms
+            return [fetch_one(j, q0, q1, r) for r in range(2)]
 
         def add_up(terms, j, q0, q1, b, copy):
             total = bank(b)
@@ -213,19 +220,19 @@ def tile_moe_sdn_glu_relu_kernel(
         unit(1, high[:2], 0, 2)()
         unit(0, high[2:], 6, 7)()
         second = unit(1, high[2:], 1, 3)
-        terms0 = fetch(0, 0, BLOCKS)
+        terms0 = [fetch_one(0, 0, BLOCKS, 0)]
         second()
+        terms0.append(fetch_one(0, 0, BLOCKS, 1))
         later = [unit(2, low, 4, 5), unit(3, low, 0, 2, True), unit(2, high, 6, 7), unit(3, high, 1, 3)]
         terms1 = fetch(1, 0, BLOCKS)
         for product in later:
             product()
-        terms2 = fetch(2, 0, 2)
+        terms2 = fetch(2, 0, 3)
         on_scalar, on_vector = nc.scalar.copy, nc.vector.tensor_copy
         add_up(terms0, 0, 0, BLOCKS, 1, on_scalar)
         add_up(terms1, 1, 0, BLOCKS, 6, on_scalar)
-        add_up(terms2, 2, 0, 2, 0, on_scalar)
+        add_up(terms2, 2, 0, 3, 0, on_scalar)
         add_up(fetch(3, 0, 2), 3, 0, 2, 4, on_scalar)
-        add_up(fetch(2, 2, 3), 2, 2, 3, 2, on_scalar)
         add_up(fetch(3, 2, 3), 3, 2, 3, 5, on_scalar)
         add_up(fetch(2, 3, 4), 2, 3, 4, 7, on_scalar)
         last = fetch(3, 3, 4)

@@ -25,6 +25,7 @@ GROUPS = E // GROUP
 GROUP_SLOTS = GROUP * C
 ROW_TILES = H // P
 BLOCKS = T // P
+GPSIMD_SLOTS = 5 * C
 EARLY_LOADS = ((0, 4), (4, 6), (6, 8))
 
 
@@ -47,12 +48,12 @@ def tile_moe_sdn_glu_relu_kernel(
         offs_sb = keep.tile([P, SLOTS // 16], U16, name="offs_sb")
         pos_sb = [keep.tile([P, T // 16], U16, name="pos%d_sb" % r) for r in range(2)]
         xw = sb("xw", [P, T], I32)
-        xs = shared.tile([P, T], U8, name="xs", align_bytes=64, offset=0)
+        xs = sb("xs", [P, T], U8)
         ws = [[sb("ws%d%d" % (m, a), [P, E, H // 2], U8) for a in range(2)] for m in range(2)]
         w2s = sb("w2s", [P, N], U8)
         w2w = sb("w2w", [P, 4 * N], U8)
         gate_sb = [sb("gate%d_sb" % r, [P, T], F32) for r in range(2)]
-        gate_cols = sb("gate_cols", [P, 2, BLOCKS], F32)
+        gate_cols = shared.tile([P, 2, BLOCKS], F32, name="gate_cols", align_bytes=64, offset=0)
         ident = sb("ident", [P, P], F32)
 
         nc.vector.memset(xs[:].bitcast(I32), 0)
@@ -105,13 +106,11 @@ def tile_moe_sdn_glu_relu_kernel(
 
         xg = [sb("xg0", [P, GROUP_SLOTS], U32), shared.tile([P, GROUP_SLOTS], U32, name="xg1", align_bytes=64, offset=0)]
         sg = [sb("sg%d" % g, [P, GROUP_SLOTS], U8) for g in range(GROUPS)]
-        xs_moved = sb("xs_moved", [P, T], U8)
-        nc.vector.tensor_copy(xs_moved[:].bitcast(I32), xs[:].bitcast(I32))
-        for g, window in enumerate((xs, xs_moved)):
+        for g in range(GROUPS):
             for half in range(2):
                 part = offs_sb[:, (2 * g + half) * 16 : (2 * g + half + 1) * 16]
                 nc.vector.tensor_copy(xg[g][:, 256 * half : 256 * (half + 1)], xw[:].bitcast(U32).indirect(part))
-                nc.vector.tensor_copy(sg[g][:, 256 * half : 256 * (half + 1)], window[:].indirect(part))
+                nc.vector.tensor_copy(sg[g][:, 256 * half : 256 * (half + 1)], xs[:].indirect(part))
 
         h = [hidden.tile([P, SLOTS], F32, name="h%d" % j, offset=at) for j, at in enumerate((8192, 2048, 0, 4096))]
         c_rows = sb("c_rows", [P, BLOCKS, 2, P, 2], BF16)
@@ -214,19 +213,34 @@ def tile_moe_sdn_glu_relu_kernel(
             nc.sync.dma_start(out[:, q0 * P : q1 * P], result[:])
 
         low, high = range(0, GROUP), range(GROUP, E)
-        unit(0, low, 0, 2, True)()
+        gated = leave(passes(0, 0, low, 0), "gated_first", RELU)
+        for pair, b in enumerate((2, 7)):
+            linear = leave(passes(1, 0, low[2 * pair : 2 * pair + 2], b), "linear_first%d" % pair, COPY)
+            slots = slice(2 * pair * C, (2 * pair + 2) * C)
+            nc.gpsimd.tensor_tensor(h[0][:, slots], linear, gated[:, slots], MULT)
         unit(1, low, 1, 3)()
         unit(0, high[:2], 4, 5)()
-        unit(1, high[:2], 0, 2)()
+        filler = unit(1, high[:2], 0, 2)
         unit(0, high[2:], 6, 7)()
+        filler()
         second = unit(1, high[2:], 1, 3)
         terms0 = [fetch_one(0, 0, BLOCKS, 0)]
         second()
         terms0.append(fetch_one(0, 0, BLOCKS, 1))
-        later = [unit(2, low, 4, 5), unit(3, low, 0, 2, True), unit(2, high, 6, 7), unit(3, high, 1, 3)]
+        third = [unit(2, low, 4, 5)]
+        gated = sb("gated_last", [P, SLOTS], F32)
+        linear = sb("linear_last", [P, GPSIMD_SLOTS], F32)
+        nc.scalar.activation(gated[:, :GROUP_SLOTS], passes(0, 3, low, 0), RELU)
+        nc.scalar.activation(linear[:, :GROUP_SLOTS], passes(1, 3, low, 2), COPY)
+        third.append(unit(2, high, 6, 7))
+        nc.scalar.activation(gated[:, GROUP_SLOTS:], passes(0, 3, high, 1), RELU)
+        sums = passes(1, 3, high, 3)
+        nc.scalar.activation(linear[:, GROUP_SLOTS:], sums[:, : GPSIMD_SLOTS - GROUP_SLOTS], COPY)
         terms1 = fetch(1, 0, BLOCKS)
-        for product in later:
+        nc.gpsimd.tensor_tensor(h[3][:, :GPSIMD_SLOTS], linear[:], gated[:, :GPSIMD_SLOTS], MULT)
+        for product in third:
             product()
+        nc.vector.tensor_tensor(h[3][:, GPSIMD_SLOTS:], sums[:, GPSIMD_SLOTS - GROUP_SLOTS :], gated[:, GPSIMD_SLOTS:], MULT)
         terms2 = fetch(2, 0, 3)
         on_scalar, on_vector = nc.scalar.copy, nc.vector.tensor_copy
         add_up(terms0, 0, 0, BLOCKS, 1, on_scalar)

@@ -25,7 +25,6 @@ GROUPS = E // GROUP
 GROUP_SLOTS = GROUP * C
 ROW_TILES = H // P
 BLOCKS = T // P
-GPSIMD_SLOTS = 5 * C
 EARLY_LOADS = ((0, 4), (4, 6), (6, 8))
 
 
@@ -88,7 +87,6 @@ def tile_moe_sdn_glu_relu_kernel(
         nc.sync.dma_start(pos_sb[1][:], pos2)
         for m in range(2):
             nc.sync.dma_start(late[m][0][:].bitcast(I32), w_words[m][:, 0:GROUP, 128:256])
-        for m in range(2):
             load_scales(ws[m][1][:].bitcast(I32), w_scales[m][:, :, 64:128])
         for m in range(2):
             nc.sync.dma_start(late[m][1][:].bitcast(I32), w_words[m][:, GROUP:E, 128:256])
@@ -112,7 +110,7 @@ def tile_moe_sdn_glu_relu_kernel(
                 nc.vector.tensor_copy(xg[g][:, 256 * half : 256 * (half + 1)], xw[:].bitcast(U32).indirect(part))
                 nc.vector.tensor_copy(sg[g][:, 256 * half : 256 * (half + 1)], xs[:].indirect(part))
 
-        h = [hidden.tile([P, SLOTS], F32, name="h%d" % j, offset=at) for j, at in enumerate((8192, 2048, 0, 4096))]
+        h = [hidden.tile([P, SLOTS], F32, name="h%d" % j, offset=at) for j, at in enumerate((8192, 1536, 0, 4096))]
         c_rows = sb("c_rows", [P, BLOCKS, 2, P, 2], BF16)
 
         def passes(m, j, experts, b):
@@ -227,20 +225,18 @@ def tile_moe_sdn_glu_relu_kernel(
         terms0 = [fetch_one(0, 0, BLOCKS, 0)]
         second()
         terms0.append(fetch_one(0, 0, BLOCKS, 1))
-        third = [unit(2, low, 4, 5)]
-        gated = sb("gated_last", [P, SLOTS], F32)
-        linear = sb("linear_last", [P, GPSIMD_SLOTS], F32)
-        nc.scalar.activation(gated[:, :GROUP_SLOTS], passes(0, 3, low, 0), RELU)
-        nc.scalar.activation(linear[:, :GROUP_SLOTS], passes(1, 3, low, 2), COPY)
-        third.append(unit(2, high, 6, 7))
-        nc.scalar.activation(gated[:, GROUP_SLOTS:], passes(0, 3, high, 1), RELU)
-        sums = passes(1, 3, high, 3)
-        nc.scalar.activation(linear[:, GROUP_SLOTS:], sums[:, : GPSIMD_SLOTS - GROUP_SLOTS], COPY)
+        gated = leave(passes(0, 2, low, 4), "gated_split", RELU)
+        sums = passes(1, 2, low, 5)
+        cut = GROUP_SLOTS - C
+        linear = leave(sums[:, cut:], "linear_split", COPY)
+        beside = unit(3, low, 0, 2, on_gpsimd=True)
+        third = [unit(2, high, 6, 7), unit(3, high, 1, 3)]
         terms1 = fetch(1, 0, BLOCKS)
-        nc.gpsimd.tensor_tensor(h[3][:, :GPSIMD_SLOTS], linear[:], gated[:, :GPSIMD_SLOTS], MULT)
+        nc.gpsimd.tensor_tensor(h[2][:, cut:GROUP_SLOTS], linear, gated[:, cut:], MULT)
+        beside()
+        nc.vector.tensor_tensor(h[2][:, :cut], sums[:, :cut], gated[:, :cut], MULT)
         for product in third:
             product()
-        nc.vector.tensor_tensor(h[3][:, GPSIMD_SLOTS:], sums[:, GPSIMD_SLOTS - GROUP_SLOTS :], gated[:, GPSIMD_SLOTS:], MULT)
         terms2 = fetch(2, 0, 3)
         on_scalar, on_vector = nc.scalar.copy, nc.vector.tensor_copy
         add_up(terms0, 0, 0, BLOCKS, 1, on_scalar)

@@ -15,6 +15,7 @@ U8 = mybir.dt.uint8
 FP8X4 = mybir.dt.float8_e4m3fn_x4
 FP4X4 = mybir.dt.float4_e2m1fn_x4
 MULT = mybir.AluOpType.mult
+ADD = mybir.AluOpType.add
 RELU = mybir.ActivationFunctionType.Relu
 COPY = mybir.ActivationFunctionType.Copy
 
@@ -36,6 +37,7 @@ def tile_moe_sdn_glu_relu_kernel(
         keep = ctx.enter_context(tc.tile_pool(name="keep", bufs=1))
         hidden = ctx.enter_context(tc.tile_pool(name="hidden", bufs=1))
         shared = ctx.enter_context(tc.tile_pool(name="shared", bufs=1))
+        reused = ctx.enter_context(tc.tile_pool(name="reused", bufs=1))
         psum = ctx.enter_context(tc.psum_pool(name="psum", bufs=1))
 
         def sb(name, shape, dtype):
@@ -53,6 +55,7 @@ def tile_moe_sdn_glu_relu_kernel(
         w2w = sb("w2w", [P, 4 * N], U8)
         gate_sb = [sb("gate%d_sb" % r, [P, T], F32) for r in range(2)]
         gate_cols = shared.tile([P, 2, BLOCKS], F32, name="gate_cols", align_bytes=64, offset=0)
+        gate_tok = [sb("gate_tok%d" % r, [P, BLOCKS], F32) for r in range(2)]
         ident = sb("ident", [P, P], F32)
 
         nc.vector.memset(xs[:].bitcast(I32), 0)
@@ -90,6 +93,9 @@ def tile_moe_sdn_glu_relu_kernel(
             load_scales(ws[m][1][:].bitcast(I32), w_scales[m][:, :, 64:128])
         for m in range(2):
             nc.sync.dma_start(late[m][1][:].bitcast(I32), w_words[m][:, GROUP:E, 128:256])
+        with nc.allow_non_contiguous_dma(reason="one gate value a token and partition"):
+            for r in range(2):
+                nc.sync.dma_start(gate_tok[r][:], gate[r, 0].rearrange("(q p) -> p q", p=P))
         nc.sync.dma_start(w2w[:].bitcast(I32), w2_words[0].rearrange("p n d -> p (n d)").bitcast(I32))
         load_scales(w2s[:].bitcast(I32), w2_scales[0].bitcast(I32))
 
@@ -110,8 +116,8 @@ def tile_moe_sdn_glu_relu_kernel(
                 nc.vector.tensor_copy(xg[g][:, 256 * half : 256 * (half + 1)], xw[:].bitcast(U32).indirect(part))
                 nc.vector.tensor_copy(sg[g][:, 256 * half : 256 * (half + 1)], xs[:].indirect(part))
 
-        h = [hidden.tile([P, SLOTS], F32, name="h%d" % j, offset=at) for j, at in enumerate((8192, 1536, 0, 4096))]
-        c_rows = sb("c_rows", [P, BLOCKS, 2, P, 2], BF16)
+        h = [hidden.tile([P, SLOTS], F32, name="h%d" % j, offset=at) for j, at in enumerate((0, 4096, 8192, 12288))]
+        c_rows = sb("c_rows", [P, BLOCKS, H], BF16)
 
         def passes(m, j, experts, b):
             sums = bank(b)
@@ -149,8 +155,9 @@ def tile_moe_sdn_glu_relu_kernel(
             engine = nc.gpsimd if on_gpsimd else nc.vector
             return lambda: engine.tensor_tensor(h[j][:, experts[0] * C : (experts[-1] + 1) * C], linear, gated, MULT)
 
-        def fetch_one(j, q0, q1, r):
-            term = sb("term%d%d%d" % (j, q0, r), [P, (q1 - q0) * P], F32)
+        def fetch_one(j, q0, q1, r, at=None):
+            name, shape = "term%d%d%d" % (j, q0, r), [P, (q1 - q0) * P]
+            term = sb(name, shape, F32) if at is None else reused.tile(shape, F32, name=name, offset=at)
             nc.vector.tensor_tensor(
                 term[:],
                 h[j][:].indirect(pos_sb[r][:, q0 * P // 16 : q1 * P // 16]),
@@ -162,31 +169,59 @@ def tile_moe_sdn_glu_relu_kernel(
         def fetch(j, q0, q1):
             return [fetch_one(j, q0, q1, r) for r in range(2)]
 
-        def add_up(terms, j, q0, q1, b, copy):
-            total = bank(b)
-            for q in range(q1 - q0):
-                for r in range(2):
+        def fetch_plain(j, q0, q1, r):
+            term = sb("term%d%d%d" % (j, q0, r), [P, (q1 - q0) * P], F32)
+            nc.scalar.activation(term[:], h[j][:].indirect(pos_sb[r][:, q0 * P // 16 : q1 * P // 16]), COPY)
+            return term
+
+        def turn(terms, total):
+            for at in range(total.shape[1] // P):
+                for r, term in enumerate(terms):
                     nc.tensor.matmul(
-                        total[:, q * P : (q + 1) * P],
-                        lhsT=terms[r][:, q * P : (q + 1) * P],
+                        total[:, at * P : (at + 1) * P],
+                        lhsT=term[:, at * P : (at + 1) * P],
                         rhs=ident[:],
                         is_transpose=True,
                         start=(r == 0),
-                        stop=(r == 1),
+                        stop=(r == len(terms) - 1),
                     )
-            view = total[:, : (q1 - q0) * P].rearrange("t (q p u e) -> t q u p e", u=2, e=2, p=32)
-            if q1 - q0 == 1:
-                copy(c_rows[:, q0, :, 32 * j : 32 * (j + 1), :], view[:, 0])
-            else:
-                for u in range(2):
-                    copy(c_rows[:, q0:q1, u, 32 * j : 32 * (j + 1), :], view[:, :, u])
+
+        def add_up(terms, j, q0, q1, b, copy):
+            total = bank(b)[:, : (q1 - q0) * P]
+            turn(terms, total)
+            copy(c_rows[:, q0:q1, j * P : (j + 1) * P], total.rearrange("t (q i) -> t q i", i=P))
+
+        def add_up_block(q, b, copy, after):
+            total = bank(b)
+            for j in (2, 3):
+                terms = [fetch_one(j, q, q + 1, r, 2048 * after + 512 * r if j == 2 else 8192 + 1024 * q + 512 * r) for r in range(2)]
+                turn(terms, total[:, (j - 2) * P : (j - 1) * P])
+            copy(c_rows[:, q, 2 * P :], total[:, : 2 * P])
+
+        def weigh(terms, j, q0, q1, banks):
+            turned = [bank(b)[:, : (q1 - q0) * P] for b in banks]
+            for r in range(2):
+                turn([terms[r]], turned[r])
+            first = reused.tile([P, (q1 - q0) * P], F32, name="first%d" % j, offset=2048 * j)
+            for q in range(q0, q1):
+                cols = slice((q - q0) * P, (q - q0 + 1) * P)
+                nc.scalar.activation(first[:, cols], turned[0][:, cols], COPY, scale=gate_tok[0][:, q : q + 1])
+
+            def finish():
+                for q in range(q0, q1):
+                    cols = slice((q - q0) * P, (q - q0 + 1) * P)
+                    nc.vector.scalar_tensor_tensor(
+                        c_rows[:, q, j * P : (j + 1) * P], turned[1][:, cols], gate_tok[1][:, q : q + 1], first[:, cols], MULT, ADD
+                    )
+
+            return finish
 
         def project(q0, q1, bank_turned, bank_acc, copy_out):
             width = (q1 - q0) * P
             turned = bank(bank_turned)
             for q in range(q1 - q0):
                 for u in range(2):
-                    words = c_rows[:, q0 + q, u].rearrange("t p e -> t (p e)").bitcast(F32)
+                    words = c_rows[:, q0 + q].bitcast(F32)[:, u::2]
                     nc.tensor.transpose(turned[:, (2 * q + u) * P : (2 * q + u + 1) * P], words, ident[:])
             c_cols = sb("c_cols%d" % q0, [P, 4 * width], BF16)
             nc.scalar.copy(
@@ -221,32 +256,23 @@ def tile_moe_sdn_glu_relu_kernel(
         filler = unit(1, high[:2], 0, 2)
         unit(0, high[2:], 6, 7)()
         filler()
-        second = unit(1, high[2:], 1, 3)
-        terms0 = [fetch_one(0, 0, BLOCKS, 0)]
-        second()
-        terms0.append(fetch_one(0, 0, BLOCKS, 1))
-        gated = leave(passes(0, 2, low, 4), "gated_split", RELU)
-        sums = passes(1, 2, low, 5)
-        cut = GROUP_SLOTS - C
-        linear = leave(sums[:, cut:], "linear_split", COPY)
-        beside = unit(3, low, 0, 2, on_gpsimd=True)
-        third = [unit(2, high, 6, 7), unit(3, high, 1, 3)]
+        unit(1, high[2:], 1, 3)()
+        terms0 = [fetch_plain(0, 0, BLOCKS, r) for r in range(2)]
+        late_products = [unit(2, low, 4, 5), unit(3, low, 0, 2), unit(2, high, 6, 7), unit(3, high, 1, 3)]
         terms1 = fetch(1, 0, BLOCKS)
-        nc.gpsimd.tensor_tensor(h[2][:, cut:GROUP_SLOTS], linear, gated[:, cut:], MULT)
-        beside()
-        nc.vector.tensor_tensor(h[2][:, :cut], sums[:, :cut], gated[:, :cut], MULT)
-        for product in third:
+        for product in late_products:
             product()
-        terms2 = fetch(2, 0, 3)
         on_scalar, on_vector = nc.scalar.copy, nc.vector.tensor_copy
-        add_up(terms0, 0, 0, BLOCKS, 1, on_scalar)
-        add_up(terms1, 1, 0, BLOCKS, 6, on_scalar)
-        add_up(terms2, 2, 0, 3, 0, on_scalar)
-        add_up(fetch(3, 0, 2), 3, 0, 2, 4, on_scalar)
-        add_up(fetch(3, 2, 3), 3, 2, 3, 5, on_scalar)
-        add_up(fetch(2, 3, 4), 2, 3, 4, 7, on_scalar)
-        last = fetch(3, 3, 4)
-        project(0, 2, 1, 6, on_scalar)
-        add_up(last, 3, 3, 4, 3, on_vector)
-        project(2, 3, 0, 4, on_scalar)
-        project(3, 4, 2, 5, on_vector)
+        finish0 = weigh(terms0, 0, 0, BLOCKS, (6, 1))
+        terms2 = [fetch_plain(2, 0, 2, r) for r in range(2)]
+        terms3 = fetch(3, 0, 2)
+        finish0()
+        add_up(terms1, 1, 0, BLOCKS, 7, on_scalar)
+        finish2 = weigh(terms2, 2, 0, 2, (0, 4))
+        add_up(terms3, 3, 0, 2, 3, on_scalar)
+        add_up_block(2, 2, on_scalar, 0)
+        finish2()
+        project(0, 2, 6, 1, on_scalar)
+        add_up_block(3, 5, on_vector, 2)
+        project(2, 3, 7, 0, on_scalar)
+        project(3, 4, 4, 3, on_vector)

@@ -117,7 +117,8 @@ def tile_moe_sdn_glu_relu_kernel(
                 nc.vector.tensor_copy(sg[g][:, 256 * half : 256 * (half + 1)], xs[:].indirect(part))
 
         h = [hidden.tile([P, SLOTS], F32, name="h%d" % j, offset=at) for j, at in enumerate((0, 4096, 8192, 12288))]
-        c_rows = sb("c_rows", [P, BLOCKS, H], BF16)
+        c_flat = sb("c_rows", [P, BLOCKS * H], BF16)
+        c_rows = c_flat[:].rearrange("t (q i) -> t q i", i=H)
 
         def passes(m, j, experts, b):
             sums = bank(b)
@@ -191,18 +192,17 @@ def tile_moe_sdn_glu_relu_kernel(
             turn(terms, total)
             copy(c_rows[:, q0:q1, j * P : (j + 1) * P], total.rearrange("t (q i) -> t q i", i=P))
 
-        def add_up_block(q, b, copy, after):
+        def add_up_block(q, b, copy):
             total = bank(b)
             for j in (2, 3):
-                terms = [fetch_one(j, q, q + 1, r, 2048 * after + 512 * r if j == 2 else 8192 + 1024 * q + 512 * r) for r in range(2)]
-                turn(terms, total[:, (j - 2) * P : (j - 1) * P])
+                turn(fetch(j, q, q + 1), total[:, (j - 2) * P : (j - 1) * P])
             copy(c_rows[:, q, 2 * P :], total[:, : 2 * P])
 
         def weigh(terms, j, q0, q1, banks):
             turned = [bank(b)[:, : (q1 - q0) * P] for b in banks]
             for r in range(2):
                 turn([terms[r]], turned[r])
-            first = reused.tile([P, (q1 - q0) * P], F32, name="first%d" % j, offset=2048 * j)
+            first = reused.tile([P, (q1 - q0) * P], F32, name="first%d" % q0, offset=512 * q0)
             for q in range(q0, q1):
                 cols = slice((q - q0) * P, (q - q0 + 1) * P)
                 nc.scalar.activation(first[:, cols], turned[0][:, cols], COPY, scale=gate_tok[0][:, q : q + 1])
@@ -221,7 +221,7 @@ def tile_moe_sdn_glu_relu_kernel(
             turned = bank(bank_turned)
             for q in range(q1 - q0):
                 for u in range(2):
-                    words = c_rows[:, q0 + q].bitcast(F32)[:, u::2]
+                    words = c_flat[:, (q0 + q) * H : (q0 + q + 1) * H].bitcast(F32)[:, u::2]
                     nc.tensor.transpose(turned[:, (2 * q + u) * P : (2 * q + u + 1) * P], words, ident[:])
             c_cols = sb("c_cols%d" % q0, [P, 4 * width], BF16)
             nc.scalar.copy(
@@ -260,19 +260,24 @@ def tile_moe_sdn_glu_relu_kernel(
         terms0 = [fetch_plain(0, 0, BLOCKS, r) for r in range(2)]
         late_products = [unit(2, low, 4, 5), unit(3, low, 0, 2), unit(2, high, 6, 7), unit(3, high, 1, 3)]
         terms1 = fetch(1, 0, BLOCKS)
+        weighed0 = [hidden.tile([P, T], F32, name="weighed%d" % r, offset=4096 + 2048 * r) for r in range(2)]
+        for r in range(2):
+            nc.gpsimd.tensor_tensor(weighed0[r][:], terms0[r][:], gate_sb[r][:], MULT)
         for product in late_products:
             product()
         on_scalar, on_vector = nc.scalar.copy, nc.vector.tensor_copy
-        finish0 = weigh(terms0, 0, 0, BLOCKS, (6, 1))
-        terms2 = [fetch_plain(2, 0, 2, r) for r in range(2)]
+        add_up(terms1, 1, 0, BLOCKS, 6, on_scalar)
+        terms2 = [fetch_plain(2, 0, 3, r) for r in range(2)]
         terms3 = fetch(3, 0, 2)
-        finish0()
-        add_up(terms1, 1, 0, BLOCKS, 7, on_scalar)
-        finish2 = weigh(terms2, 2, 0, 2, (0, 4))
-        add_up(terms3, 3, 0, 2, 3, on_scalar)
-        add_up_block(2, 2, on_scalar, 0)
-        finish2()
-        project(0, 2, 6, 1, on_scalar)
-        add_up_block(3, 5, on_vector, 2)
-        project(2, 3, 7, 0, on_scalar)
-        project(3, 4, 4, 3, on_vector)
+        add_up(weighed0, 0, 0, BLOCKS, 1, on_scalar)
+        finish_pair = weigh([term[:, : 2 * P] for term in terms2], 2, 0, 2, (0, 4))
+        add_up(terms3, 3, 0, 2, 7, on_scalar)
+        finish_last = weigh([term[:, 2 * P :] for term in terms2], 2, 2, 3, (2, 5))
+        add_up_block(3, 3, on_scalar)
+        finish_pair()
+        last = [fetch_one(3, 2, 3, r, 512 * r) for r in range(2)]
+        finish_last()
+        project(0, 2, 6, 0, on_scalar)
+        add_up(last, 3, 2, 3, 1, on_vector)
+        project(3, 4, 7, 4, on_scalar)
+        project(2, 3, 2, 3, on_vector)

@@ -117,8 +117,15 @@ def tile_moe_sdn_glu_relu_kernel(
                 nc.vector.tensor_copy(sg[g][:, 256 * half : 256 * (half + 1)], xs[:].indirect(part))
 
         h = [hidden.tile([P, SLOTS], F32, name="h%d" % j, offset=at) for j, at in enumerate((0, 4096, 8192, 12288))]
-        c_flat = sb("c_rows", [P, BLOCKS * H], BF16)
-        c_rows = c_flat[:].rearrange("t (q i) -> t q i", i=H)
+        c_flat = [reused.tile([P, 2 * H], BF16, name="c_rows%d" % a, offset=2048 * a) for a in range(BLOCKS // 2)]
+
+        def c_rows(q0, q1, j):
+            rows = c_flat[q0 // 2][:].rearrange("t (q u j x) -> t q u j x", u=2, j=ROW_TILES, x=64)
+            return rows[:, q0 % 2 : q0 % 2 + q1 - q0, :, j]
+
+        def parted(total):
+            return total.rearrange("t (q u x) -> t q u x", u=2, x=64)
+
 
         def passes(m, j, experts, b):
             sums = bank(b)
@@ -170,8 +177,9 @@ def tile_moe_sdn_glu_relu_kernel(
         def fetch(j, q0, q1):
             return [fetch_one(j, q0, q1, r) for r in range(2)]
 
-        def fetch_plain(j, q0, q1, r):
-            term = sb("term%d%d%d" % (j, q0, r), [P, (q1 - q0) * P], F32)
+        def fetch_plain(j, q0, q1, r, at=None):
+            name, shape = "term%d%d%d" % (j, q0, r), [P, (q1 - q0) * P]
+            term = sb(name, shape, F32) if at is None else reused.tile(shape, F32, name=name, offset=at)
             nc.scalar.activation(term[:], h[j][:].indirect(pos_sb[r][:, q0 * P // 16 : q1 * P // 16]), COPY)
             return term
 
@@ -179,7 +187,7 @@ def tile_moe_sdn_glu_relu_kernel(
             for at in range(total.shape[1] // P):
                 for r, term in enumerate(terms):
                     nc.tensor.matmul(
-                        total[:, at * P : (at + 1) * P],
+                        total[:, at * P : (at + 1) * P].rearrange("t (u p e) -> t p u e", u=2, e=2),
                         lhsT=term[:, at * P : (at + 1) * P],
                         rhs=ident[:],
                         is_transpose=True,
@@ -190,19 +198,13 @@ def tile_moe_sdn_glu_relu_kernel(
         def add_up(terms, j, q0, q1, b, copy):
             total = bank(b)[:, : (q1 - q0) * P]
             turn(terms, total)
-            copy(c_rows[:, q0:q1, j * P : (j + 1) * P], total.rearrange("t (q i) -> t q i", i=P))
+            for q in range(q0, q1, 2):
+                end = min(q + 2, q1)
+                copy(c_rows(q, end, j), parted(total)[:, q - q0 : end - q0])
 
-        def add_up_block(q, b, copy):
-            total = bank(b)
-            for j in (2, 3):
-                turn(fetch(j, q, q + 1), total[:, (j - 2) * P : (j - 1) * P])
-            copy(c_rows[:, q, 2 * P :], total[:, : 2 * P])
-
-        def weigh(terms, j, q0, q1, banks):
-            turned = [bank(b)[:, : (q1 - q0) * P] for b in banks]
-            for r in range(2):
-                turn([terms[r]], turned[r])
-            first = reused.tile([P, (q1 - q0) * P], F32, name="first%d" % q0, offset=512 * q0)
+        def weigh(turned0, turned1, j, q0, q1):
+            turned = [turned0, turned1]
+            first = sb("first%d" % q0, [P, (q1 - q0) * P], F32)
             for q in range(q0, q1):
                 cols = slice((q - q0) * P, (q - q0 + 1) * P)
                 nc.scalar.activation(first[:, cols], turned[0][:, cols], COPY, scale=gate_tok[0][:, q : q + 1])
@@ -211,27 +213,34 @@ def tile_moe_sdn_glu_relu_kernel(
                 for q in range(q0, q1):
                     cols = slice((q - q0) * P, (q - q0 + 1) * P)
                     nc.vector.scalar_tensor_tensor(
-                        c_rows[:, q, j * P : (j + 1) * P], turned[1][:, cols], gate_tok[1][:, q : q + 1], first[:, cols], MULT, ADD
+                        c_rows(q, q + 1, j)[:, 0],
+                        parted(turned[1][:, cols])[:, 0],
+                        gate_tok[1][:, q : q + 1],
+                        parted(first[:, cols])[:, 0],
+                        MULT,
+                        ADD,
                     )
 
             return finish
 
-        def project(q0, q1, bank_turned, bank_acc, copy_out):
+        def turn_back(q0, q1, b, c_cols, copy):
             width = (q1 - q0) * P
-            turned = bank(bank_turned)
+            turned = bank(b)
             for q in range(q1 - q0):
                 for u in range(2):
-                    words = c_flat[:, (q0 + q) * H : (q0 + q + 1) * H].bitcast(F32)[:, u::2]
+                    words = c_flat[q0 // 2][:, (q0 % 2 + q) * H + 256 * u : (q0 % 2 + q) * H + 256 * (u + 1)].bitcast(F32)
                     nc.tensor.transpose(turned[:, (2 * q + u) * P : (2 * q + u + 1) * P], words, ident[:])
-            c_cols = sb("c_cols%d" % q0, [P, 4 * width], BF16)
-            nc.scalar.copy(
-                c_cols[:].bitcast(F32).rearrange("p (q t u) -> p q t u", u=2, t=P),
+            copy(
+                c_cols.bitcast(F32).rearrange("p (q t u) -> p q t u", u=2, t=P),
                 turned[:, : 2 * width].rearrange("p (q u t) -> p q t u", u=2, t=P),
             )
+
+        def project(c_cols, q0, q1, b):
+            width = (q1 - q0) * P
             codes = sb("codes%d" % q0, [P, width], U32)
             scales = sb("scales%d" % q0, [P, width], U8)
             nc.vector.quantize_mx(out=codes[:].bitcast(FP8X4), scales=scales[:], in_=c_cols[:])
-            acc = bank(bank_acc)
+            acc = bank(b)
             nc.tensor.matmul_mx(
                 out=acc[:, :width],
                 lhsT=w2w[:].bitcast(FP8X4),
@@ -241,8 +250,11 @@ def tile_moe_sdn_glu_relu_kernel(
                 start=True,
                 stop=True,
             )
-            result = sb("result%d" % q0, [P, width], F32)
-            copy_out(result[:], acc[:, :width])
+            return acc[:, :width]
+
+        def store(acc, q0, q1, copy):
+            result = sb("result%d" % q0, [P, (q1 - q0) * P], F32)
+            copy(result[:], acc)
             nc.sync.dma_start(out[:, q0 * P : q1 * P], result[:])
 
         low, high = range(0, GROUP), range(GROUP, E)
@@ -266,18 +278,35 @@ def tile_moe_sdn_glu_relu_kernel(
         for product in late_products:
             product()
         on_scalar, on_vector = nc.scalar.copy, nc.vector.tensor_copy
-        add_up(terms1, 1, 0, BLOCKS, 6, on_scalar)
-        terms2 = [fetch_plain(2, 0, 3, r) for r in range(2)]
-        terms3 = fetch(3, 0, 2)
-        add_up(weighed0, 0, 0, BLOCKS, 1, on_scalar)
-        finish_pair = weigh([term[:, : 2 * P] for term in terms2], 2, 0, 2, (0, 4))
-        add_up(terms3, 3, 0, 2, 7, on_scalar)
-        finish_last = weigh([term[:, 2 * P :] for term in terms2], 2, 2, 3, (2, 5))
-        add_up_block(3, 3, on_scalar)
+        sums1 = bank(6)
+        turn(terms1, sums1[:])
+        on_scalar(c_rows(0, 2, 1), parted(sums1[:])[:, :2])
+        terms2 = [fetch_plain(2, 0, BLOCKS, 0, 2048), fetch_plain(2, 0, BLOCKS, 1)]
+        terms3 = [fetch(3, q, q + 2) for q in (0, 2)]
+        sums0 = bank(1)
+        turn(weighed0, sums0[:])
+        half = 2 * P
+        mixed = [bank(b) for b in (0, 2, 4, 5)]
+        turn([terms2[0][:, :half]], mixed[0][:, :half])
+        turn([terms2[0][:, half:]], mixed[1][:, :half])
+        sums3 = bank(3)
+        turn(terms3[0], sums3[:, :half])
+        turn([terms2[1][:, :half]], mixed[2][:, :half])
+        turn([terms2[1][:, half:]], mixed[3][:, :half])
+        turn(terms3[1], mixed[3][:, half:])
+        finish_pair = weigh(mixed[0], mixed[2], 2, 0, 2)
+        on_scalar(c_rows(0, 2, 0), parted(sums0[:])[:, :2])
+        finish_last = weigh(mixed[1], mixed[3], 2, 2, 4)
+        on_scalar(c_rows(2, 4, 1), parted(sums1[:])[:, 2:])
+        on_scalar(c_rows(2, 4, 0), parted(sums0[:])[:, 2:])
+        on_vector(c_rows(0, 2, 3), parted(sums3[:, :half]))
         finish_pair()
-        last = [fetch_one(3, 2, 3, r, 512 * r) for r in range(2)]
         finish_last()
-        project(0, 2, 6, 0, on_scalar)
-        add_up(last, 3, 2, 3, 1, on_vector)
-        project(3, 4, 7, 4, on_scalar)
-        project(2, 3, 2, 3, on_vector)
+        on_vector(c_rows(2, 4, 3), parted(mixed[3][:, half:]))
+        parts = ((0, 2, 7, 0, on_scalar), (2, 3, 3, 4, on_vector), (3, 4, 6, 2, on_scalar))
+        cols = [sb("c_cols%d" % q0, [P, 4 * P * (q1 - q0)], BF16) for q0, q1, b, acc, copy in parts]
+        for at, (q0, q1, b, acc, copy) in enumerate(parts):
+            turn_back(q0, q1, b, cols[at][:], copy)
+        sums = [project(cols[at], q0, q1, acc) for at, (q0, q1, b, acc, copy) in enumerate(parts)]
+        for at, (q0, q1, b, acc, copy) in enumerate(parts):
+            store(sums[at], q0, q1, copy)

@@ -117,14 +117,14 @@ def tile_moe_sdn_glu_relu_kernel(
                 nc.vector.tensor_copy(sg[g][:, 256 * half : 256 * (half + 1)], xs[:].indirect(part))
 
         h = [hidden.tile([P, SLOTS], F32, name="h%d" % j, offset=at) for j, at in enumerate((0, 4096, 8192, 12288))]
-        c_flat = [reused.tile([P, 2 * H], BF16, name="c_rows%d" % a, offset=2048 * a) for a in range(BLOCKS // 2)]
+        c_flat = [reused.tile([P, 2 * H], BF16, name="c_rows%d" % a, offset=1024 + 2048 * a) for a in range(BLOCKS // 2)]
 
         def c_rows(q0, q1, j):
-            rows = c_flat[q0 // 2][:].rearrange("t (q u j x) -> t q u j x", u=2, j=ROW_TILES, x=64)
-            return rows[:, q0 % 2 : q0 % 2 + q1 - q0, :, j]
+            rows = c_flat[q0 // 2][:].rearrange("t (q j i) -> t q j i", j=ROW_TILES, i=P)
+            return rows[:, q0 % 2 : q0 % 2 + q1 - q0, j]
 
         def parted(total):
-            return total.rearrange("t (q u x) -> t q u x", u=2, x=64)
+            return total.rearrange("t (q i) -> t q i", i=P)
 
 
         def passes(m, j, experts, b):
@@ -187,7 +187,7 @@ def tile_moe_sdn_glu_relu_kernel(
             for at in range(total.shape[1] // P):
                 for r, term in enumerate(terms):
                     nc.tensor.matmul(
-                        total[:, at * P : (at + 1) * P].rearrange("t (u p e) -> t p u e", u=2, e=2),
+                        total[:, at * P : (at + 1) * P],
                         lhsT=term[:, at * P : (at + 1) * P],
                         rhs=ident[:],
                         is_transpose=True,
@@ -228,7 +228,7 @@ def tile_moe_sdn_glu_relu_kernel(
             turned = bank(b)
             for q in range(q1 - q0):
                 for u in range(2):
-                    words = c_flat[q0 // 2][:, (q0 % 2 + q) * H + 256 * u : (q0 % 2 + q) * H + 256 * (u + 1)].bitcast(F32)
+                    words = c_flat[q0 // 2][:, (q0 % 2 + q) * H : (q0 % 2 + q + 1) * H].bitcast(F32)[:, u::2]
                     nc.tensor.transpose(turned[:, (2 * q + u) * P : (2 * q + u + 1) * P], words, ident[:])
             copy(
                 c_cols.bitcast(F32).rearrange("p (q t u) -> p q t u", u=2, t=P),
@@ -270,7 +270,7 @@ def tile_moe_sdn_glu_relu_kernel(
         filler()
         unit(1, high[2:], 1, 3)()
         terms0 = [fetch_plain(0, 0, BLOCKS, r) for r in range(2)]
-        late_products = [unit(2, low, 4, 5), unit(3, low, 0, 2), unit(2, high, 6, 7), unit(3, high, 1, 3)]
+        late_products = [unit(2, low, 4, 5), unit(2, high, 0, 2), unit(3, low, 6, 7), unit(3, high, 1, 3)]
         terms1 = fetch(1, 0, BLOCKS)
         weighed0 = [hidden.tile([P, T], F32, name="weighed%d" % r, offset=4096 + 2048 * r) for r in range(2)]
         for r in range(2):
@@ -278,35 +278,39 @@ def tile_moe_sdn_glu_relu_kernel(
         for product in late_products:
             product()
         on_scalar, on_vector = nc.scalar.copy, nc.vector.tensor_copy
-        sums1 = bank(6)
-        turn(terms1, sums1[:])
-        on_scalar(c_rows(0, 2, 1), parted(sums1[:])[:, :2])
         terms2 = [fetch_plain(2, 0, BLOCKS, 0, 2048), fetch_plain(2, 0, BLOCKS, 1)]
         terms3 = [fetch(3, q, q + 2) for q in (0, 2)]
-        sums0 = bank(1)
-        turn(weighed0, sums0[:])
         half = 2 * P
-        mixed = [bank(b) for b in (0, 2, 4, 5)]
+        early_sums = [bank(b) for b in (0, 1)]
+        for j, terms in ((1, terms1), (0, weighed0)):
+            for a in range(2):
+                turn([term[:, a * half : (a + 1) * half] for term in terms], early_sums[a][:, j * half : (j + 1) * half])
+
+        def leave_early(a):
+            rows = c_flat[a][:].rearrange("t (q j i) -> t j q i", j=ROW_TILES, i=P)[:, :2]
+            on_scalar(rows, early_sums[a][:].rearrange("t (j q i) -> t j q i", j=2, i=P))
+
+        mixed = [bank(b) for b in (6, 2, 4, 5)]
         turn([terms2[0][:, :half]], mixed[0][:, :half])
         turn([terms2[0][:, half:]], mixed[1][:, :half])
         sums3 = bank(3)
         turn(terms3[0], sums3[:, :half])
         turn([terms2[1][:, :half]], mixed[2][:, :half])
         turn([terms2[1][:, half:]], mixed[3][:, :half])
-        turn(terms3[1], mixed[3][:, half:])
         finish_pair = weigh(mixed[0], mixed[2], 2, 0, 2)
-        on_scalar(c_rows(0, 2, 0), parted(sums0[:])[:, :2])
+        sums3b = bank(6)
+        turn(terms3[1], sums3b[:, :half])
+        on_scalar(c_rows(0, 2, 3), parted(sums3[:, :half]))
+        leave_early(0)
         finish_last = weigh(mixed[1], mixed[3], 2, 2, 4)
-        on_scalar(c_rows(2, 4, 1), parted(sums1[:])[:, 2:])
-        on_scalar(c_rows(2, 4, 0), parted(sums0[:])[:, 2:])
-        on_vector(c_rows(0, 2, 3), parted(sums3[:, :half]))
+        leave_early(1)
         finish_pair()
+        on_vector(c_rows(2, 4, 3), parted(sums3b[:, :half]))
         finish_last()
-        on_vector(c_rows(2, 4, 3), parted(mixed[3][:, half:]))
-        parts = ((0, 2, 7, 0, on_scalar), (2, 3, 3, 4, on_vector), (3, 4, 6, 2, on_scalar))
+        parts = ((0, 2, 3, 0, on_vector), (2, 3, 7, 4, on_scalar), (3, 4, 6, 2, on_scalar))
         cols = [sb("c_cols%d" % q0, [P, 4 * P * (q1 - q0)], BF16) for q0, q1, b, acc, copy in parts]
         for at, (q0, q1, b, acc, copy) in enumerate(parts):
             turn_back(q0, q1, b, cols[at][:], copy)
         sums = [project(cols[at], q0, q1, acc) for at, (q0, q1, b, acc, copy) in enumerate(parts)]
         for at, (q0, q1, b, acc, copy) in enumerate(parts):
-            store(sums[at], q0, q1, copy)
+            store(sums[at], q0, q1, (on_scalar, on_vector, on_scalar)[at])

@@ -20,13 +20,19 @@ RELU = mybir.ActivationFunctionType.Relu
 COPY = mybir.ActivationFunctionType.Copy
 
 P = 128
+BANK = 512
 SLOTS = E * C
 GROUP = 4
 GROUPS = E // GROUP
 GROUP_SLOTS = GROUP * C
 ROW_TILES = H // P
 BLOCKS = T // P
+PAIR = 2 * P
+GATHER = 2 * C
+HALF_ROW = H
 EARLY_LOADS = ((0, 4), (4, 6), (6, 8))
+H_BYTES = 4 * SLOTS
+TERM_BYTES = 4 * T
 
 
 def tile_moe_sdn_glu_relu_kernel(
@@ -39,12 +45,13 @@ def tile_moe_sdn_glu_relu_kernel(
         shared = ctx.enter_context(tc.tile_pool(name="shared", bufs=1))
         reused = ctx.enter_context(tc.tile_pool(name="reused", bufs=1))
         psum = ctx.enter_context(tc.psum_pool(name="psum", bufs=1))
+        on_scalar, on_vector = nc.scalar.copy, nc.vector.tensor_copy
 
         def sb(name, shape, dtype):
             return keep.tile(shape, dtype, name=name, align_bytes=64)
 
         def bank(b):
-            return psum.tile([P, 512], F32, name="bank%d" % b)
+            return psum.tile([P, BANK], F32, name="bank%d" % b)
 
         offs_sb = keep.tile([P, SLOTS // 16], U16, name="offs_sb")
         pos_sb = [keep.tile([P, T // 16], U16, name="pos%d_sb" % r) for r in range(2)]
@@ -53,19 +60,13 @@ def tile_moe_sdn_glu_relu_kernel(
         ws = [[sb("ws%d%d" % (m, a), [P, E, H // 2], U8) for a in range(2)] for m in range(2)]
         w2s = sb("w2s", [P, N], U8)
         w2w = sb("w2w", [P, 4 * N], U8)
-        gate_sb = [sb("gate%d_sb" % r, [P, T], F32) for r in range(2)]
-        gate_cols = shared.tile([P, 2, BLOCKS], F32, name="gate_cols", align_bytes=64, offset=0)
+        gate_rows = [sb("gate_rows%d" % r, [P, T], F32) for r in range(2)]
+        gate_runs = shared.tile([P, 2, BLOCKS], F32, name="gate_runs", align_bytes=64, offset=0)
         gate_tok = [sb("gate_tok%d" % r, [P, BLOCKS], F32) for r in range(2)]
         ident = sb("ident", [P, P], F32)
 
         nc.vector.memset(xs[:].bitcast(I32), 0)
-        for m in range(2):
-            nc.vector.memset(ws[m][0][:, :GROUP].bitcast(I32), 0)
-            nc.gpsimd.memset(ws[m][0][:, GROUP:].bitcast(I32), 0)
         make_identity(nc, ident[:])
-        for m in range(2):
-            nc.vector.memset(ws[m][1][:].bitcast(I32), 0)
-        nc.vector.memset(w2s[:].bitcast(I32), 0)
 
         def load_scales(plane, rows, queues=(nc.sync,) * 4):
             for r, queue in enumerate(queues):
@@ -73,26 +74,27 @@ def tile_moe_sdn_glu_relu_kernel(
 
         w_words = [w.rearrange("e s p n -> p (e s) n").bitcast(I32) for w in (w1_words, w3_words)]
         w_scales = [w.rearrange("e s b n -> b (e s) n").bitcast(I32) for w in (w1_scales, w3_scales)]
-        early = [[sb("we%d%d" % (m, e0), [P, e1 - e0, 512], U8) for e0, e1 in EARLY_LOADS] for m in range(2)]
-        late = [[sb("wl%d%d" % (m, g), [P, GROUP, 512], U8) for g in range(GROUPS)] for m in range(2)]
+        early = [[sb("we%d%d" % (m, e0), [P, e1 - e0, HALF_ROW], U8) for e0, e1 in EARLY_LOADS] for m in range(2)]
+        late = [[sb("wl%d%d" % (m, g), [P, GROUP, HALF_ROW], U8) for g in range(GROUPS)] for m in range(2)]
+        first_words, last_words = slice(0, HALF_ROW // 4), slice(HALF_ROW // 4, HALF_ROW // 2)
+        first_scales, last_scales = slice(0, H // 8), slice(H // 8, H // 4)
 
         nc.sync.dma_start(xw[:], x_words[0].rearrange("p t d -> p (t d)").bitcast(I32))
         nc.sync.dma_start(offs_sb[:], offs)
         load_scales(xs[:].bitcast(I32), x_scales[0].bitcast(I32), (nc.sync, nc.scalar) * 2)
-        nc.sync.dma_start(gate_cols[:], gate[:, 0].rearrange("r (p q) -> p r q", q=BLOCKS))
+        nc.sync.dma_start(gate_runs[:], gate[:, 0].rearrange("r (p n) -> p r n", n=BLOCKS))
         for m in range(2):
-            nc.sync.dma_start(early[m][0][:].bitcast(I32), w_words[m][:, 0:GROUP, 0:128])
-            load_scales(ws[m][0][:].bitcast(I32), w_scales[m][:, :, 0:64])
+            nc.sync.dma_start(early[m][0][:].bitcast(I32), w_words[m][:, 0:GROUP, first_words])
+            load_scales(ws[m][0][:].bitcast(I32), w_scales[m][:, :, first_scales])
         for at, (e0, e1) in list(enumerate(EARLY_LOADS))[1:]:
             for m in range(2):
-                nc.sync.dma_start(early[m][at][:].bitcast(I32), w_words[m][:, e0:e1, 0:128])
+                nc.sync.dma_start(early[m][at][:].bitcast(I32), w_words[m][:, e0:e1, first_words])
         nc.sync.dma_start(pos_sb[0][:], pos1)
         nc.sync.dma_start(pos_sb[1][:], pos2)
         for m in range(2):
-            nc.sync.dma_start(late[m][0][:].bitcast(I32), w_words[m][:, 0:GROUP, 128:256])
-            load_scales(ws[m][1][:].bitcast(I32), w_scales[m][:, :, 64:128])
-        for m in range(2):
-            nc.sync.dma_start(late[m][1][:].bitcast(I32), w_words[m][:, GROUP:E, 128:256])
+            nc.sync.dma_start(late[m][0][:].bitcast(I32), w_words[m][:, 0:GROUP, last_words])
+            load_scales(ws[m][1][:].bitcast(I32), w_scales[m][:, :, last_scales])
+            nc.sync.dma_start(late[m][1][:].bitcast(I32), w_words[m][:, GROUP:E, last_words])
         with nc.allow_non_contiguous_dma(reason="one gate value a token and partition"):
             for r in range(2):
                 nc.sync.dma_start(gate_tok[r][:], gate[r, 0].rearrange("(q p) -> p q", p=P))
@@ -101,31 +103,31 @@ def tile_moe_sdn_glu_relu_kernel(
 
         for r in range(2):
             spread = bank(7 - r)
-            for q in range(BLOCKS):
-                column = gate_cols[:, r, q : q + 1]
-                nc.tensor.transpose(spread[:, q * P : (q + 1) * P], column.to_broadcast([P, P]), ident[:])
+            for n in range(BLOCKS):
+                column = gate_runs[:, r, n : n + 1]
+                nc.tensor.transpose(spread[:, n * P : (n + 1) * P], column.to_broadcast([P, P]), ident[:])
             nc.scalar.activation(
-                gate_sb[r][:].rearrange("p (n q) -> p n q", q=BLOCKS), spread[:].rearrange("p (q n) -> p n q", q=BLOCKS), COPY
+                gate_rows[r][:].rearrange("p (c n) -> p c n", n=BLOCKS), spread[:].rearrange("p (n c) -> p c n", n=BLOCKS), COPY
             )
 
         xg = [sb("xg0", [P, GROUP_SLOTS], U32), shared.tile([P, GROUP_SLOTS], U32, name="xg1", align_bytes=64, offset=0)]
         sg = [sb("sg%d" % g, [P, GROUP_SLOTS], U8) for g in range(GROUPS)]
         for g in range(GROUPS):
-            for half in range(2):
-                part = offs_sb[:, (2 * g + half) * 16 : (2 * g + half + 1) * 16]
-                nc.vector.tensor_copy(xg[g][:, 256 * half : 256 * (half + 1)], xw[:].bitcast(U32).indirect(part))
-                nc.vector.tensor_copy(sg[g][:, 256 * half : 256 * (half + 1)], xs[:].indirect(part))
+            for start in range(0, GROUP_SLOTS, GATHER):
+                entries = offs_sb[:, (g * GROUP_SLOTS + start) // 16 : (g * GROUP_SLOTS + start + GATHER) // 16]
+                nc.vector.tensor_copy(xg[g][:, start : start + GATHER], xw[:].bitcast(U32).indirect(entries))
+                nc.vector.tensor_copy(sg[g][:, start : start + GATHER], xs[:].indirect(entries))
 
-        h = [hidden.tile([P, SLOTS], F32, name="h%d" % j, offset=at) for j, at in enumerate((0, 4096, 8192, 12288))]
-        c_flat = [reused.tile([P, 2 * H], BF16, name="c_rows%d" % a, offset=1024 + 2048 * a) for a in range(BLOCKS // 2)]
+        h = [hidden.tile([P, SLOTS], F32, name="h%d" % j, offset=j * H_BYTES) for j in range(ROW_TILES)]
+        c_pairs = [
+            reused.tile([P, 2 * H], BF16, name="c_pair%d" % a, offset=TERM_BYTES // 2 + a * TERM_BYTES) for a in range(BLOCKS // 2)
+        ]
 
-        def c_rows(q0, q1, j):
-            rows = c_flat[q0 // 2][:].rearrange("t (q j i) -> t q j i", j=ROW_TILES, i=P)
-            return rows[:, q0 % 2 : q0 % 2 + q1 - q0, j]
+        def c_rows(a):
+            return c_pairs[a][:].rearrange("t (q j i) -> t j q i", j=ROW_TILES, i=P)
 
-        def parted(total):
-            return total.rearrange("t (q i) -> t q i", i=P)
-
+        def by_block(sums):
+            return sums.rearrange("t (q i) -> t q i", i=P)
 
         def passes(m, j, experts, b):
             sums = bank(b)
@@ -136,7 +138,7 @@ def tile_moe_sdn_glu_relu_kernel(
                     row = early[m][load][:, e - EARLY_LOADS[load][0]]
                 else:
                     row = late[m][g][:, el]
-                words = row[:, 256 * (j % 2) : 256 * (j % 2 + 1)]
+                words = row[:, 2 * P * (j % 2) : 2 * P * (j % 2 + 1)]
                 slots = slice(el * C, (el + 1) * C)
                 nc.tensor.matmul_mx(
                     out=sums[:, at * C : (at + 1) * C],
@@ -154,40 +156,28 @@ def tile_moe_sdn_glu_relu_kernel(
             nc.scalar.activation(kept[:], sums, func)
             return kept[:]
 
-        def unit(j, experts, bank_a, bank_b, on_gpsimd=False):
-            name = "%d_%d" % (j, experts[0])
-            gated = leave(passes(0, j, experts, bank_a), "gated" + name, RELU)
-            linear = passes(1, j, experts, bank_b)
-            if on_gpsimd:
-                linear = leave(linear, "linear" + name, COPY)
-            engine = nc.gpsimd if on_gpsimd else nc.vector
-            return lambda: engine.tensor_tensor(h[j][:, experts[0] * C : (experts[-1] + 1) * C], linear, gated, MULT)
+        def unit(j, experts, bank_w1, bank_w3, name):
+            gated = leave(passes(0, j, experts, bank_w1), name, RELU)
+            linear = passes(1, j, experts, bank_w3)
+            return lambda: nc.vector.tensor_tensor(h[j][:, experts[0] * C : (experts[-1] + 1) * C], linear, gated, MULT)
 
-        def fetch_one(j, q0, q1, r, at=None):
-            name, shape = "term%d%d%d" % (j, q0, r), [P, (q1 - q0) * P]
-            term = sb(name, shape, F32) if at is None else reused.tile(shape, F32, name=name, offset=at)
-            nc.vector.tensor_tensor(
-                term[:],
-                h[j][:].indirect(pos_sb[r][:, q0 * P // 16 : q1 * P // 16]),
-                gate_sb[r][:, q0 * P : q1 * P],
-                MULT,
-            )
+        def fetch_weighed(j, t0, t1):
+            terms = []
+            for r in range(2):
+                term = sb("term%d_%d_%d" % (j, t0, r), [P, t1 - t0], F32)
+                nc.vector.tensor_tensor(term[:], h[j][:].indirect(pos_sb[r][:, t0 // 16 : t1 // 16]), gate_rows[r][:, t0:t1], MULT)
+                terms.append(term)
+            return terms
+
+        def fetch_plain(j, r, term):
+            nc.scalar.activation(term[:], h[j][:].indirect(pos_sb[r][:]), COPY)
             return term
 
-        def fetch(j, q0, q1):
-            return [fetch_one(j, q0, q1, r) for r in range(2)]
-
-        def fetch_plain(j, q0, q1, r, at=None):
-            name, shape = "term%d%d%d" % (j, q0, r), [P, (q1 - q0) * P]
-            term = sb(name, shape, F32) if at is None else reused.tile(shape, F32, name=name, offset=at)
-            nc.scalar.activation(term[:], h[j][:].indirect(pos_sb[r][:, q0 * P // 16 : q1 * P // 16]), COPY)
-            return term
-
-        def turn(terms, total):
-            for at in range(total.shape[1] // P):
+        def turn(terms, sums):
+            for at in range(sums.shape[1] // P):
                 for r, term in enumerate(terms):
                     nc.tensor.matmul(
-                        total[:, at * P : (at + 1) * P],
+                        sums[:, at * P : (at + 1) * P],
                         lhsT=term[:, at * P : (at + 1) * P],
                         rhs=ident[:],
                         is_transpose=True,
@@ -195,44 +185,29 @@ def tile_moe_sdn_glu_relu_kernel(
                         stop=(r == len(terms) - 1),
                     )
 
-        def add_up(terms, j, q0, q1, b, copy):
-            total = bank(b)[:, : (q1 - q0) * P]
-            turn(terms, total)
-            for q in range(q0, q1, 2):
-                end = min(q + 2, q1)
-                copy(c_rows(q, end, j), parted(total)[:, q - q0 : end - q0])
-
-        def weigh(turned0, turned1, j, q0, q1):
-            turned = [turned0, turned1]
-            first = sb("first%d" % q0, [P, (q1 - q0) * P], F32)
-            for q in range(q0, q1):
-                cols = slice((q - q0) * P, (q - q0 + 1) * P)
-                nc.scalar.activation(first[:, cols], turned[0][:, cols], COPY, scale=gate_tok[0][:, q : q + 1])
+        def weigh(turned0, turned1, a):
+            first = sb("first%d" % a, [P, PAIR], F32)
+            for q in range(2):
+                cols = slice(q * P, (q + 1) * P)
+                nc.scalar.activation(first[:, cols], turned0[:, cols], COPY, scale=gate_tok[0][:, 2 * a + q : 2 * a + q + 1])
 
             def finish():
-                for q in range(q0, q1):
-                    cols = slice((q - q0) * P, (q - q0 + 1) * P)
-                    nc.vector.scalar_tensor_tensor(
-                        c_rows(q, q + 1, j)[:, 0],
-                        parted(turned[1][:, cols])[:, 0],
-                        gate_tok[1][:, q : q + 1],
-                        parted(first[:, cols])[:, 0],
-                        MULT,
-                        ADD,
-                    )
+                for q in range(2):
+                    cols = slice(q * P, (q + 1) * P)
+                    weight = gate_tok[1][:, 2 * a + q : 2 * a + q + 1]
+                    nc.vector.scalar_tensor_tensor(c_rows(a)[:, 2, q], turned1[:, cols], weight, first[:, cols], MULT, ADD)
 
             return finish
 
         def turn_back(q0, q1, b, c_cols, copy):
-            width = (q1 - q0) * P
             turned = bank(b)
-            for q in range(q1 - q0):
+            for at, q in enumerate(range(q0, q1)):
                 for u in range(2):
-                    words = c_flat[q0 // 2][:, (q0 % 2 + q) * H : (q0 % 2 + q + 1) * H].bitcast(F32)[:, u::2]
-                    nc.tensor.transpose(turned[:, (2 * q + u) * P : (2 * q + u + 1) * P], words, ident[:])
+                    words = c_pairs[q // 2][:, q % 2 * H : (q % 2 + 1) * H].bitcast(F32)[:, u::2]
+                    nc.tensor.transpose(turned[:, (2 * at + u) * P : (2 * at + u + 1) * P], words, ident[:])
             copy(
-                c_cols.bitcast(F32).rearrange("p (q t u) -> p q t u", u=2, t=P),
-                turned[:, : 2 * width].rearrange("p (q u t) -> p q t u", u=2, t=P),
+                c_cols[:].bitcast(F32).rearrange("p (q t u) -> p q t u", u=2, t=P),
+                turned[:, : 2 * P * (q1 - q0)].rearrange("p (q u t) -> p q t u", u=2, t=P),
             )
 
         def project(c_cols, q0, q1, b):
@@ -258,59 +233,68 @@ def tile_moe_sdn_glu_relu_kernel(
             nc.sync.dma_start(out[:, q0 * P : q1 * P], result[:])
 
         low, high = range(0, GROUP), range(GROUP, E)
-        gated = leave(passes(0, 0, low, 0), "gated_first", RELU)
+        gated = leave(passes(0, 0, low, 0), "gated0_low", RELU)
         for pair, b in enumerate((2, 7)):
-            linear = leave(passes(1, 0, low[2 * pair : 2 * pair + 2], b), "linear_first%d" % pair, COPY)
+            linear = leave(passes(1, 0, low[2 * pair : 2 * pair + 2], b), "linear0_%d" % pair, COPY)
             slots = slice(2 * pair * C, (2 * pair + 2) * C)
             nc.gpsimd.tensor_tensor(h[0][:, slots], linear, gated[:, slots], MULT)
-        unit(1, low, 1, 3)()
-        unit(0, high[:2], 4, 5)()
-        filler = unit(1, high[:2], 0, 2)
-        unit(0, high[2:], 6, 7)()
-        filler()
-        unit(1, high[2:], 1, 3)()
-        terms0 = [fetch_plain(0, 0, BLOCKS, r) for r in range(2)]
-        late_products = [unit(2, low, 4, 5), unit(2, high, 0, 2), unit(3, low, 6, 7), unit(3, high, 1, 3)]
-        terms1 = fetch(1, 0, BLOCKS)
-        weighed0 = [hidden.tile([P, T], F32, name="weighed%d" % r, offset=4096 + 2048 * r) for r in range(2)]
+        unit(1, low, 1, 3, "gated1_low")()
+        unit(0, high[:2], 4, 5, "gated0_third")()
+        product1_third = unit(1, high[:2], 0, 2, "gated1_third")
+        unit(0, high[2:], 6, 7, "gated0_fourth")()
+        product1_third()
+        unit(1, high[2:], 1, 3, "gated1_fourth")()
+
+        terms0 = [fetch_plain(0, r, sb("term0_%d" % r, [P, T], F32)) for r in range(2)]
+        late_products = [unit(2, low, 4, 5, "gated_low"), unit(2, high, 0, 2, "gated2_high"), unit(3, high, 1, 3, "gated3_high")]
+        terms1 = fetch_weighed(1, 0, T)
+        weighed0 = [hidden.tile([P, T], F32, name="weighed%d" % r, offset=H_BYTES + r * TERM_BYTES) for r in range(2)]
         for r in range(2):
-            nc.gpsimd.tensor_tensor(weighed0[r][:], terms0[r][:], gate_sb[r][:], MULT)
+            nc.gpsimd.tensor_tensor(weighed0[r][:], terms0[r][:], gate_rows[r][:], MULT)
         for product in late_products:
             product()
-        on_scalar, on_vector = nc.scalar.copy, nc.vector.tensor_copy
-        terms2 = [fetch_plain(2, 0, BLOCKS, 0, 2048), fetch_plain(2, 0, BLOCKS, 1)]
-        terms3 = [fetch(3, q, q + 2) for q in (0, 2)]
-        half = 2 * P
-        early_sums = [bank(b) for b in (0, 1)]
+        unit(3, low, 6, 7, "gated_low")()
+
+        terms2 = [
+            fetch_plain(2, 0, reused.tile([P, T], F32, name="term2_0", offset=TERM_BYTES)),
+            fetch_plain(2, 1, sb("term2_1", [P, T], F32)),
+        ]
+        terms3 = [fetch_weighed(3, a * PAIR, (a + 1) * PAIR) for a in range(2)]
+
+        sums01 = [bank(b) for b in (5, 2)]
         for j, terms in ((1, terms1), (0, weighed0)):
             for a in range(2):
-                turn([term[:, a * half : (a + 1) * half] for term in terms], early_sums[a][:, j * half : (j + 1) * half])
+                turn([term[:, a * PAIR : (a + 1) * PAIR] for term in terms], sums01[a][:, j * PAIR : (j + 1) * PAIR])
 
-        def leave_early(a):
-            rows = c_flat[a][:].rearrange("t (q j i) -> t j q i", j=ROW_TILES, i=P)[:, :2]
-            on_scalar(rows, early_sums[a][:].rearrange("t (j q i) -> t j q i", j=2, i=P))
+        def leave01(a):
+            on_scalar(c_rows(a)[:, :2], sums01[a][:].rearrange("t (j q i) -> t j q i", j=2, i=P))
 
-        mixed = [bank(b) for b in (6, 2, 4, 5)]
-        turn([terms2[0][:, :half]], mixed[0][:, :half])
-        turn([terms2[0][:, half:]], mixed[1][:, :half])
-        sums3 = bank(3)
-        turn(terms3[0], sums3[:, :half])
-        turn([terms2[1][:, :half]], mixed[2][:, :half])
-        turn([terms2[1][:, half:]], mixed[3][:, :half])
-        finish_pair = weigh(mixed[0], mixed[2], 2, 0, 2)
-        sums3b = bank(6)
-        turn(terms3[1], sums3b[:, :half])
-        on_scalar(c_rows(0, 2, 3), parted(sums3[:, :half]))
-        leave_early(0)
-        finish_last = weigh(mixed[1], mixed[3], 2, 2, 4)
-        leave_early(1)
-        finish_pair()
-        on_vector(c_rows(2, 4, 3), parted(sums3b[:, :half]))
-        finish_last()
-        parts = ((0, 2, 3, 0, on_vector), (2, 3, 7, 4, on_scalar), (3, 4, 6, 2, on_scalar))
-        cols = [sb("c_cols%d" % q0, [P, 4 * P * (q1 - q0)], BF16) for q0, q1, b, acc, copy in parts]
-        for at, (q0, q1, b, acc, copy) in enumerate(parts):
-            turn_back(q0, q1, b, cols[at][:], copy)
-        sums = [project(cols[at], q0, q1, acc) for at, (q0, q1, b, acc, copy) in enumerate(parts)]
-        for at, (q0, q1, b, acc, copy) in enumerate(parts):
-            store(sums[at], q0, q1, (on_scalar, on_vector, on_scalar)[at])
+        turned2 = [[bank(b)[:, :PAIR] for b in banks] for banks in ((4, 0), (6, 1))]
+        for a in range(2):
+            turn([terms2[0][:, a * PAIR : (a + 1) * PAIR]], turned2[0][a])
+        sums3_first = bank(3)[:, :PAIR]
+        turn(terms3[0], sums3_first)
+        for a in range(2):
+            turn([terms2[1][:, a * PAIR : (a + 1) * PAIR]], turned2[1][a])
+        finish_first = weigh(turned2[0][0], turned2[1][0], 0)
+        sums3_second = bank(4)[:, :PAIR]
+        turn(terms3[1], sums3_second)
+        on_scalar(c_rows(0)[:, 3], by_block(sums3_first))
+        leave01(0)
+        finish_second = weigh(turned2[0][1], turned2[1][1], 1)
+        leave01(1)
+        finish_first()
+        on_vector(c_rows(1)[:, 3], by_block(sums3_second))
+        finish_second()
+
+        parts = (
+            (0, 2, 3, 5, on_vector, on_scalar),
+            (2, 3, 7, 6, on_scalar, on_scalar),
+            (3, 4, 4, 0, on_scalar, on_vector),
+        )
+        cols = [sb("c_cols%d" % part[0], [P, 4 * P * (part[1] - part[0])], BF16) for part in parts]
+        for c_cols, (q0, q1, bank_turned, bank_acc, interleave, copy_out) in zip(cols, parts):
+            turn_back(q0, q1, bank_turned, c_cols, interleave)
+        results = [project(c_cols, part[0], part[1], part[3]) for c_cols, part in zip(cols, parts)]
+        for acc, (q0, q1, bank_turned, bank_acc, interleave, copy_out) in zip(results, parts):
+            store(acc, q0, q1, copy_out)

@@ -32,7 +32,7 @@ GATHER = 2 * C
 HALF_ROW = H
 EARLY_LOADS = ((0, 4), (4, 6), (6, 8))
 H_BYTES = 4 * SLOTS
-TERM_BYTES = 4 * T
+SUMMED = 3 * P
 
 
 def tile_moe_sdn_glu_relu_kernel(
@@ -43,7 +43,6 @@ def tile_moe_sdn_glu_relu_kernel(
         keep = ctx.enter_context(tc.tile_pool(name="keep", bufs=1))
         hidden = ctx.enter_context(tc.tile_pool(name="hidden", bufs=1))
         shared = ctx.enter_context(tc.tile_pool(name="shared", bufs=1))
-        reused = ctx.enter_context(tc.tile_pool(name="reused", bufs=1))
         psum = ctx.enter_context(tc.psum_pool(name="psum", bufs=1))
         on_scalar, on_vector = nc.scalar.copy, nc.vector.tensor_copy
 
@@ -65,9 +64,6 @@ def tile_moe_sdn_glu_relu_kernel(
         gate_tok = [sb("gate_tok%d" % r, [P, BLOCKS], F32) for r in range(2)]
         ident = sb("ident", [P, P], F32)
 
-        nc.vector.memset(xs[:].bitcast(I32), 0)
-        make_identity(nc, ident[:])
-
         def load_scales(plane, rows, queues=(nc.sync,) * 4):
             for r, queue in enumerate(queues):
                 queue.dma_start(plane[r:P:32], rows[r:16:4])
@@ -79,6 +75,8 @@ def tile_moe_sdn_glu_relu_kernel(
         first_words, last_words = slice(0, HALF_ROW // 4), slice(HALF_ROW // 4, HALF_ROW // 2)
         first_scales, last_scales = slice(0, H // 8), slice(H // 8, H // 4)
 
+        nc.vector.memset(xs[:].bitcast(I32), 0)
+        make_identity(nc, ident[:])
         nc.sync.dma_start(xw[:], x_words[0].rearrange("p t d -> p (t d)").bitcast(I32))
         nc.sync.dma_start(offs_sb[:], offs)
         load_scales(xs[:].bitcast(I32), x_scales[0].bitcast(I32), (nc.sync, nc.scalar) * 2)
@@ -119,15 +117,6 @@ def tile_moe_sdn_glu_relu_kernel(
                 nc.vector.tensor_copy(sg[g][:, start : start + GATHER], xs[:].indirect(entries))
 
         h = [hidden.tile([P, SLOTS], F32, name="h%d" % j, offset=j * H_BYTES) for j in range(ROW_TILES)]
-        c_pairs = [
-            reused.tile([P, 2 * H], BF16, name="c_pair%d" % a, offset=TERM_BYTES // 2 + a * TERM_BYTES) for a in range(BLOCKS // 2)
-        ]
-
-        def c_rows(a):
-            return c_pairs[a][:].rearrange("t (q j i) -> t j q i", j=ROW_TILES, i=P)
-
-        def by_block(sums):
-            return sums.rearrange("t (q i) -> t q i", i=P)
 
         def passes(m, j, experts, b):
             sums = bank(b)
@@ -161,60 +150,126 @@ def tile_moe_sdn_glu_relu_kernel(
             linear = passes(1, j, experts, bank_w3)
             return lambda: nc.vector.tensor_tensor(h[j][:, experts[0] * C : (experts[-1] + 1) * C], linear, gated, MULT)
 
-        def fetch_weighed(j, t0, t1):
-            terms = []
-            for r in range(2):
-                term = sb("term%d_%d_%d" % (j, t0, r), [P, t1 - t0], F32)
-                nc.vector.tensor_tensor(term[:], h[j][:].indirect(pos_sb[r][:, t0 // 16 : t1 // 16]), gate_rows[r][:, t0:t1], MULT)
-                terms.append(term)
-            return terms
+        def entries_of(r, t0, t1):
+            return pos_sb[r][:, t0 // 16 : t1 // 16]
 
-        def fetch_plain(j, r, term):
-            nc.scalar.activation(term[:], h[j][:].indirect(pos_sb[r][:]), COPY)
+        def fetch_weighed(j, r, t0, t1):
+            term = sb("term%d_%d_%d" % (j, r, t0), [P, t1 - t0], F32)
+            nc.vector.tensor_tensor(term[:], h[j][:].indirect(entries_of(r, t0, t1)), gate_rows[r][:, t0:t1], MULT)
+            return [term[:, at : at + P] for at in range(0, t1 - t0, P)]
+
+        def fetch_plain(j, r, t0, t1):
+            term = sb("term%d_%d_%d" % (j, r, t0), [P, t1 - t0], F32)
+            nc.scalar.activation(term[:], h[j][:].indirect(entries_of(r, t0, t1)), COPY)
             return term
 
-        def turn(terms, sums):
-            for at in range(sums.shape[1] // P):
-                for r, term in enumerate(terms):
-                    nc.tensor.matmul(
-                        sums[:, at * P : (at + 1) * P],
-                        lhsT=term[:, at * P : (at + 1) * P],
-                        rhs=ident[:],
-                        is_transpose=True,
-                        start=(r == 0),
-                        stop=(r == len(terms) - 1),
-                    )
+        def turn(piece, into, start, stop):
+            nc.tensor.matmul(into, lhsT=piece, rhs=ident[:], is_transpose=True, start=start, stop=stop)
 
-        def weigh(turned0, turned1, a):
-            first = sb("first%d" % a, [P, PAIR], F32)
-            for q in range(2):
-                cols = slice(q * P, (q + 1) * P)
-                nc.scalar.activation(first[:, cols], turned0[:, cols], COPY, scale=gate_tok[0][:, 2 * a + q : 2 * a + q + 1])
+        low, high = range(0, GROUP), range(GROUP, E)
+        gated = leave(passes(0, 0, low, 0), "gated0_low", RELU)
+        for pair, b in enumerate((2, 7)):
+            linear = leave(passes(1, 0, low[2 * pair : 2 * pair + 2], b), "linear0_%d" % pair, COPY)
+            slots = slice(2 * pair * C, (2 * pair + 2) * C)
+            nc.gpsimd.tensor_tensor(h[0][:, slots], linear, gated[:, slots], MULT)
+        unit(1, low, 1, 3, "gated1_low")()
+        unit(0, high[:2], 4, 5, "gated0_third")()
+        product1_third = unit(1, high[:2], 0, 2, "gated1_third")
+        unit(0, high[2:], 6, 7, "gated0_fourth")()
+        product1_third()
+        unit(1, high[2:], 1, 3, "gated1_fourth")()
 
-            def finish():
-                for q in range(2):
-                    cols = slice(q * P, (q + 1) * P)
-                    weight = gate_tok[1][:, 2 * a + q : 2 * a + q + 1]
-                    nc.vector.scalar_tensor_tensor(c_rows(a)[:, 2, q], turned1[:, cols], weight, first[:, cols], MULT, ADD)
+        terms0 = [fetch_plain(0, r, 0, T) for r in range(2)]
+        late_products = [unit(3, low, 4, 5, "gated3_low"), unit(3, high, 0, 2, "gated3_high"), unit(2, high, 1, 3, "gated2_high")]
+        terms1 = [fetch_weighed(1, r, 0, T) for r in range(2)]
+        weighed = hidden.tile([P, T], F32, name="weighed0", offset=H_BYTES)
+        nc.gpsimd.tensor_tensor(weighed[:], terms0[0][:], gate_rows[0][:], MULT)
+        weighed0 = [weighed]
+        late_products[0]()
+        weighed = sb("gated3_low", [P, T], F32)
+        nc.gpsimd.tensor_tensor(weighed[:], terms0[1][:], gate_rows[1][:], MULT)
+        weighed0.append(weighed)
+        late_products[1]()
+        late_products[2]()
+        unit(2, low, 6, 7, "gated3_high")()
 
-            return finish
+        first3 = fetch_plain(3, 0, 0, T)
+        second3 = [fetch_plain(3, 1, a * PAIR, (a + 1) * PAIR) for a in range(2)]
+        terms2 = [[], []]
+        for t0, t1 in ((0, PAIR), (PAIR, PAIR + P), (PAIR + P, T)):
+            for r in range(2):
+                terms2[r].extend(fetch_weighed(2, r, t0, t1))
 
-        def turn_back(q0, q1, b, c_cols, copy):
+        sums = [bank(b) for b in (2, 3, 6, 7)]
+        for q in range(BLOCKS):
+            for r in range(2):
+                turn(terms1[r][q], sums[q][:, P : 2 * P], r == 0, False)
+            turn(weighed0[0][:, q * P : (q + 1) * P], sums[q][:, :P], False, False)
+        for q in range(BLOCKS):
+            turn(weighed0[1][:, q * P : (q + 1) * P], sums[q][:, :P], False, False)
+        turned3 = [bank(5), bank(4)]
+        for q in range(BLOCKS):
+            turn(first3[:, q * P : (q + 1) * P], turned3[0][:, q * P : (q + 1) * P], True, True)
+
+        def turn2(q):
+            for r in range(2):
+                turn(terms2[r][q], sums[q][:, 2 * P : 3 * P], False, r == 1)
+
+        def turn3(q):
+            turn(second3[q // 2][:, q % 2 * P : (q % 2 + 1) * P], turned3[1][:, q * P : (q + 1) * P], True, True)
+
+        turn2(0)
+        turn2(1)
+        turn3(0)
+        turn3(1)
+        turn2(2)
+        turn3(2)
+        turn3(3)
+        turn2(3)
+
+        c_rows = [sb("c_rows%d" % q, [P, H], BF16) for q in range(BLOCKS)]
+        firsts = [sb("first%d" % q, [P, P], F32) for q in range(BLOCKS)]
+
+        def parted(cols):
+            return cols.rearrange("t (p u e) -> t u p e", u=2, e=2)
+
+        def rows_of(q):
+            return c_rows[q][:].rearrange("t (u p e) -> t u p e", u=2, e=2)
+
+        def weigh_first(q):
+            nc.scalar.activation(firsts[q][:], turned3[0][:, q * P : (q + 1) * P], COPY, scale=gate_tok[0][:, q : q + 1])
+
+        def add_second(q):
+            for u in range(2):
+                nc.vector.scalar_tensor_tensor(
+                    rows_of(q)[:, u, SUMMED // 4 :],
+                    parted(turned3[1][:, q * P : (q + 1) * P])[:, u],
+                    gate_tok[1][:, q : q + 1],
+                    parted(firsts[q][:])[:, u],
+                    MULT,
+                    ADD,
+                )
+
+        def leave_sums(q, copy):
+            copy(rows_of(q)[:, :, : SUMMED // 4], parted(sums[q][:, :SUMMED]))
+
+        c_cols = sb("c_cols", [P, 4 * T], BF16)
+
+        def turn_back(q, b):
             turned = bank(b)
-            for at, q in enumerate(range(q0, q1)):
-                for u in range(2):
-                    words = c_pairs[q // 2][:, q % 2 * H : (q % 2 + 1) * H].bitcast(F32)[:, u::2]
-                    nc.tensor.transpose(turned[:, (2 * at + u) * P : (2 * at + u + 1) * P], words, ident[:])
-            copy(
-                c_cols[:].bitcast(F32).rearrange("p (q t u) -> p q t u", u=2, t=P),
-                turned[:, : 2 * P * (q1 - q0)].rearrange("p (q u t) -> p q t u", u=2, t=P),
-            )
+            for u in range(2):
+                nc.tensor.transpose(turned[:, u * P : (u + 1) * P], c_rows[q][:].bitcast(F32)[:, u * P : (u + 1) * P], ident[:])
+            return turned
 
-        def project(c_cols, q0, q1, b):
+        def interleave(q, turned, copy):
+            words = c_cols[:].bitcast(F32)[:, q * PAIR : (q + 1) * PAIR]
+            copy(words.rearrange("p (t u) -> p t u", u=2), turned[:, :PAIR].rearrange("p (u t) -> p t u", u=2))
+
+        def project(q0, q1, b):
             width = (q1 - q0) * P
             codes = sb("codes%d" % q0, [P, width], U32)
             scales = sb("scales%d" % q0, [P, width], U8)
-            nc.vector.quantize_mx(out=codes[:].bitcast(FP8X4), scales=scales[:], in_=c_cols[:])
+            nc.vector.quantize_mx(out=codes[:].bitcast(FP8X4), scales=scales[:], in_=c_cols[:, 4 * P * q0 : 4 * P * q1])
             acc = bank(b)
             nc.tensor.matmul_mx(
                 out=acc[:, :width],
@@ -232,69 +287,22 @@ def tile_moe_sdn_glu_relu_kernel(
             copy(result[:], acc)
             nc.sync.dma_start(out[:, q0 * P : q1 * P], result[:])
 
-        low, high = range(0, GROUP), range(GROUP, E)
-        gated = leave(passes(0, 0, low, 0), "gated0_low", RELU)
-        for pair, b in enumerate((2, 7)):
-            linear = leave(passes(1, 0, low[2 * pair : 2 * pair + 2], b), "linear0_%d" % pair, COPY)
-            slots = slice(2 * pair * C, (2 * pair + 2) * C)
-            nc.gpsimd.tensor_tensor(h[0][:, slots], linear, gated[:, slots], MULT)
-        unit(1, low, 1, 3, "gated1_low")()
-        unit(0, high[:2], 4, 5, "gated0_third")()
-        product1_third = unit(1, high[:2], 0, 2, "gated1_third")
-        unit(0, high[2:], 6, 7, "gated0_fourth")()
-        product1_third()
-        unit(1, high[2:], 1, 3, "gated1_fourth")()
-
-        terms0 = [fetch_plain(0, r, sb("term0_%d" % r, [P, T], F32)) for r in range(2)]
-        late_products = [unit(2, low, 4, 5, "gated_low"), unit(2, high, 0, 2, "gated2_high"), unit(3, high, 1, 3, "gated3_high")]
-        terms1 = fetch_weighed(1, 0, T)
-        weighed0 = [hidden.tile([P, T], F32, name="weighed%d" % r, offset=H_BYTES + r * TERM_BYTES) for r in range(2)]
-        for r in range(2):
-            nc.gpsimd.tensor_tensor(weighed0[r][:], terms0[r][:], gate_rows[r][:], MULT)
-        for product in late_products:
-            product()
-        unit(3, low, 6, 7, "gated_low")()
-
-        terms2 = [
-            fetch_plain(2, 0, reused.tile([P, T], F32, name="term2_0", offset=TERM_BYTES)),
-            fetch_plain(2, 1, sb("term2_1", [P, T], F32)),
-        ]
-        terms3 = [fetch_weighed(3, a * PAIR, (a + 1) * PAIR) for a in range(2)]
-
-        sums01 = [bank(b) for b in (5, 2)]
-        for j, terms in ((1, terms1), (0, weighed0)):
-            for a in range(2):
-                turn([term[:, a * PAIR : (a + 1) * PAIR] for term in terms], sums01[a][:, j * PAIR : (j + 1) * PAIR])
-
-        def leave01(a):
-            on_scalar(c_rows(a)[:, :2], sums01[a][:].rearrange("t (j q i) -> t j q i", j=2, i=P))
-
-        turned2 = [[bank(b)[:, :PAIR] for b in banks] for banks in ((4, 0), (6, 1))]
-        for a in range(2):
-            turn([terms2[0][:, a * PAIR : (a + 1) * PAIR]], turned2[0][a])
-        sums3_first = bank(3)[:, :PAIR]
-        turn(terms3[0], sums3_first)
-        for a in range(2):
-            turn([terms2[1][:, a * PAIR : (a + 1) * PAIR]], turned2[1][a])
-        finish_first = weigh(turned2[0][0], turned2[1][0], 0)
-        sums3_second = bank(4)[:, :PAIR]
-        turn(terms3[1], sums3_second)
-        on_scalar(c_rows(0)[:, 3], by_block(sums3_first))
-        leave01(0)
-        finish_second = weigh(turned2[0][1], turned2[1][1], 1)
-        leave01(1)
-        finish_first()
-        on_vector(c_rows(1)[:, 3], by_block(sums3_second))
-        finish_second()
-
-        parts = (
-            (0, 2, 3, 5, on_vector, on_scalar),
-            (2, 3, 7, 6, on_scalar, on_scalar),
-            (3, 4, 4, 0, on_scalar, on_vector),
-        )
-        cols = [sb("c_cols%d" % part[0], [P, 4 * P * (part[1] - part[0])], BF16) for part in parts]
-        for c_cols, (q0, q1, bank_turned, bank_acc, interleave, copy_out) in zip(cols, parts):
-            turn_back(q0, q1, bank_turned, c_cols, interleave)
-        results = [project(c_cols, part[0], part[1], part[3]) for c_cols, part in zip(cols, parts)]
-        for acc, (q0, q1, bank_turned, bank_acc, interleave, copy_out) in zip(results, parts):
-            store(acc, q0, q1, copy_out)
+        weigh_first(0)
+        weigh_first(1)
+        leave_sums(0, on_scalar)
+        add_second(0)
+        add_second(1)
+        leave_sums(1, on_vector)
+        weigh_first(2)
+        weigh_first(3)
+        leave_sums(2, on_scalar)
+        add_second(2)
+        add_second(3)
+        leave_sums(3, on_vector)
+        turned = [turn_back(q, b) for q, b in enumerate((0, 1, 2, 3))]
+        for q, copy in enumerate((on_scalar, on_scalar, on_scalar, on_scalar)):
+            interleave(q, turned[q], copy)
+        parts = ((0, 2, 5, on_vector), (2, 3, 4, on_vector), (3, 4, 6, on_scalar))
+        results = [project(q0, q1, b) for q0, q1, b, copy in parts]
+        for acc, (q0, q1, b, copy) in zip(results, parts):
+            store(acc, q0, q1, copy)

@@ -145,10 +145,20 @@ def tile_moe_sdn_glu_relu_kernel(
             nc.scalar.activation(kept[:], sums, func)
             return kept[:]
 
-        def unit(j, experts, bank_w1, bank_w3, name):
-            gated = leave(passes(0, j, experts, bank_w1), name, RELU)
+        def unit(j, experts, bank_w1, bank_w3, name, step=GROUP_SLOTS):
+            sums = passes(0, j, experts, bank_w1)
+            width = sums.shape[1]
+            pieces = [slice(at, min(at + step, width)) for at in range(0, width, step)]
+            gated = sb(name, [P, width], F32)
+            for piece in pieces:
+                nc.scalar.activation(gated[:, piece], sums[:, piece], RELU)
             linear = passes(1, j, experts, bank_w3)
-            return lambda: nc.vector.tensor_tensor(h[j][:, experts[0] * C : (experts[-1] + 1) * C], linear, gated, MULT)
+
+            def multiply():
+                for piece in pieces:
+                    nc.vector.tensor_tensor(h[j][:, experts[0] * C :][:, piece], linear[:, piece], gated[:, piece], MULT)
+
+            return multiply
 
         def entries_of(r, t0, t1):
             return pos_sb[r][:, t0 // 16 : t1 // 16]
@@ -180,7 +190,11 @@ def tile_moe_sdn_glu_relu_kernel(
         unit(1, high[2:], 1, 3, "gated1_fourth")()
 
         terms0 = [fetch_plain(0, r, 0, T) for r in range(2)]
-        late_products = [unit(3, low, 4, 5, "gated3_low"), unit(3, high, 0, 2, "gated3_high"), unit(2, high, 1, 3, "gated2_high")]
+        late_products = [
+            unit(3, low, 4, 5, "gated3_low", GATHER),
+            unit(3, high, 0, 2, "gated3_high", GATHER),
+            unit(2, high, 1, 3, "gated2_high", GATHER),
+        ]
         terms1 = [fetch_weighed(1, r, 0, T) for r in range(2)]
         weighed = hidden.tile([P, T], F32, name="weighed0", offset=H_BYTES)
         nc.gpsimd.tensor_tensor(weighed[:], terms0[0][:], gate_rows[0][:], MULT)
@@ -191,7 +205,7 @@ def tile_moe_sdn_glu_relu_kernel(
         weighed0.append(weighed)
         late_products[1]()
         late_products[2]()
-        unit(2, low, 6, 7, "gated3_high")()
+        unit(2, low, 6, 7, "gated3_high", GATHER)()
 
         first3 = fetch_plain(3, 0, 0, T)
         second3 = [fetch_plain(3, 1, a * PAIR, (a + 1) * PAIR) for a in range(2)]
@@ -292,7 +306,7 @@ def tile_moe_sdn_glu_relu_kernel(
         leave_sums(0, on_scalar)
         add_second(0)
         add_second(1)
-        leave_sums(1, on_vector)
+        leave_sums(1, on_scalar)
         weigh_first(2)
         weigh_first(3)
         leave_sums(2, on_scalar)
@@ -300,7 +314,7 @@ def tile_moe_sdn_glu_relu_kernel(
         add_second(3)
         leave_sums(3, on_vector)
         turned = [turn_back(q, b) for q, b in enumerate((0, 1, 2, 3))]
-        for q, copy in enumerate((on_scalar, on_scalar, on_scalar, on_scalar)):
+        for q, copy in enumerate((on_scalar, on_vector, on_scalar, on_scalar)):
             interleave(q, turned[q], copy)
         parts = ((0, 2, 5, on_vector), (2, 3, 4, on_vector), (3, 4, 6, on_scalar))
         results = [project(q0, q1, b) for q0, q1, b, copy in parts]

@@ -145,11 +145,13 @@ def tile_moe_sdn_glu_relu_kernel(
             nc.scalar.activation(kept[:], sums, func)
             return kept[:]
 
-        def unit(j, experts, bank_w1, bank_w3, name, step=GROUP_SLOTS):
+        def on_hidden(name, at):
+            return hidden.tile([P, T], F32, name=name, offset=at * H_BYTES // 2)
+
+        def unit(j, experts, bank_w1, bank_w3, gated, step=GROUP_SLOTS):
             sums = passes(0, j, experts, bank_w1)
             width = sums.shape[1]
             pieces = [slice(at, min(at + step, width)) for at in range(0, width, step)]
-            gated = sb(name, [P, width], F32)
             for piece in pieces:
                 nc.scalar.activation(gated[:, piece], sums[:, piece], RELU)
             linear = passes(1, j, experts, bank_w3)
@@ -182,30 +184,28 @@ def tile_moe_sdn_glu_relu_kernel(
             linear = leave(passes(1, 0, low[2 * pair : 2 * pair + 2], b), "linear0_%d" % pair, COPY)
             slots = slice(2 * pair * C, (2 * pair + 2) * C)
             nc.gpsimd.tensor_tensor(h[0][:, slots], linear, gated[:, slots], MULT)
-        unit(1, low, 1, 3, "gated1_low")()
-        unit(0, high[:2], 4, 5, "gated0_third")()
-        product1_third = unit(1, high[:2], 0, 2, "gated1_third")
-        unit(0, high[2:], 6, 7, "gated0_fourth")()
+        unit(1, low, 1, 3, sb("gated1_low", [P, GROUP_SLOTS], F32))()
+        unit(0, high[:2], 4, 5, sb("gated0_third", [P, GATHER], F32))()
+        product1_third = unit(1, high[:2], 0, 2, sb("gated1_third", [P, GATHER], F32))
+        unit(0, high[2:], 6, 7, sb("gated0_fourth", [P, GATHER], F32))()
         product1_third()
-        unit(1, high[2:], 1, 3, "gated1_fourth")()
+        unit(1, high[2:], 1, 3, sb("gated1_fourth", [P, GATHER], F32))()
 
         terms0 = [fetch_plain(0, r, 0, T) for r in range(2)]
-        late_products = [
-            unit(3, low, 4, 5, "gated3_low", GATHER),
-            unit(3, high, 0, 2, "gated3_high", GATHER),
-            unit(2, high, 1, 3, "gated2_high", GATHER),
-        ]
         terms1 = [fetch_weighed(1, r, 0, T) for r in range(2)]
-        weighed = hidden.tile([P, T], F32, name="weighed0", offset=H_BYTES)
-        nc.gpsimd.tensor_tensor(weighed[:], terms0[0][:], gate_rows[0][:], MULT)
-        weighed0 = [weighed]
+        late_products = [
+            unit(3, low, 4, 5, on_hidden("gated3_low", 0), GATHER),
+            unit(3, high, 0, 2, on_hidden("gated3_high", 1), GATHER),
+            unit(2, high, 1, 3, on_hidden("gated2_high", 3), GATHER),
+        ]
+        weighed0 = [on_hidden("weighed_first", 2)]
+        nc.gpsimd.tensor_tensor(weighed0[0][:], terms0[0][:], gate_rows[0][:], MULT)
         late_products[0]()
-        weighed = sb("gated3_low", [P, T], F32)
-        nc.gpsimd.tensor_tensor(weighed[:], terms0[1][:], gate_rows[1][:], MULT)
-        weighed0.append(weighed)
+        weighed0.append(on_hidden("weighed_second", 0))
+        nc.gpsimd.tensor_tensor(weighed0[1][:], terms0[1][:], gate_rows[1][:], MULT)
         late_products[1]()
         late_products[2]()
-        unit(2, low, 6, 7, "gated3_high", GATHER)()
+        unit(2, low, 6, 7, on_hidden("gated2_low", 1), GATHER)()
 
         first3 = fetch_plain(3, 0, 0, T)
         second3 = [fetch_plain(3, 1, a * PAIR, (a + 1) * PAIR) for a in range(2)]
@@ -214,20 +214,29 @@ def tile_moe_sdn_glu_relu_kernel(
             for r in range(2):
                 terms2[r].extend(fetch_weighed(2, r, t0, t1))
 
-        sums = [bank(b) for b in (2, 3, 6, 7)]
-        for q in range(BLOCKS):
-            for r in range(2):
-                turn(terms1[r][q], sums[q][:, P : 2 * P], r == 0, False)
-            turn(weighed0[0][:, q * P : (q + 1) * P], sums[q][:, :P], False, False)
-        for q in range(BLOCKS):
-            turn(weighed0[1][:, q * P : (q + 1) * P], sums[q][:, :P], False, False)
-        turned3 = [bank(5), bank(4)]
+        sums01 = [bank(5), bank(2)]
+
+        def turn01(j, pieces, start, stop):
+            for q in range(BLOCKS):
+                at = (2 * j + q % 2) * P
+                turn(pieces[q], sums01[q // 2][:, at : at + P], start and q % 2 == 0, stop and q % 2 == 1)
+
+        def blocks_of(term):
+            return [term[:, q * P : (q + 1) * P] for q in range(BLOCKS)]
+
+        turn01(1, terms1[0], True, False)
+        turn01(1, terms1[1], False, False)
+        turn01(0, blocks_of(weighed0[0]), False, False)
+        turn01(0, blocks_of(weighed0[1]), False, True)
+        turned3 = [bank(4), bank(0)]
+        first_pair = bank(1)
+        sums2 = [first_pair[:, :P], first_pair[:, P:PAIR], bank(6)[:, :P], bank(3)[:, :P]]
         for q in range(BLOCKS):
             turn(first3[:, q * P : (q + 1) * P], turned3[0][:, q * P : (q + 1) * P], True, True)
 
         def turn2(q):
             for r in range(2):
-                turn(terms2[r][q], sums[q][:, 2 * P : 3 * P], False, r == 1)
+                turn(terms2[r][q], sums2[q], r == 0, r == 1)
 
         def turn3(q):
             turn(second3[q // 2][:, q % 2 * P : (q % 2 + 1) * P], turned3[1][:, q * P : (q + 1) * P], True, True)
@@ -241,14 +250,14 @@ def tile_moe_sdn_glu_relu_kernel(
         turn3(3)
         turn2(3)
 
-        c_rows = [sb("c_rows%d" % q, [P, H], BF16) for q in range(BLOCKS)]
+        c_pairs = [sb("c_pair%d" % a, [P, 2 * H], BF16) for a in range(2)]
         firsts = [sb("first%d" % q, [P, P], F32) for q in range(BLOCKS)]
 
         def parted(cols):
             return cols.rearrange("t (p u e) -> t u p e", u=2, e=2)
 
         def rows_of(q):
-            return c_rows[q][:].rearrange("t (u p e) -> t u p e", u=2, e=2)
+            return c_pairs[q // 2][:, q % 2 * H : (q % 2 + 1) * H].rearrange("t (u p e) -> t u p e", u=2, e=2)
 
         def weigh_first(q):
             nc.scalar.activation(firsts[q][:], turned3[0][:, q * P : (q + 1) * P], COPY, scale=gate_tok[0][:, q : q + 1])
@@ -264,15 +273,23 @@ def tile_moe_sdn_glu_relu_kernel(
                     ADD,
                 )
 
-        def leave_sums(q, copy):
-            copy(rows_of(q)[:, :, : SUMMED // 4], parted(sums[q][:, :SUMMED]))
+        def leave01(a, copy):
+            rows = c_pairs[a][:].rearrange("t (q u j w) -> t j q u w", q=2, u=2, j=ROW_TILES)[:, :2]
+            copy(rows, sums01[a][:].rearrange("t (jq p u e) -> t jq u p e", jq=4, u=2, e=2))
+
+        def leave2_pair(copy):
+            rows = c_pairs[0][:].rearrange("t (q u j w) -> t j q u w", q=2, u=2, j=ROW_TILES)[:, 2]
+            copy(rows, first_pair[:, :PAIR].rearrange("t (q p u e) -> t q u p e", q=2, u=2, e=2))
+
+        def leave2(q, copy):
+            copy(rows_of(q)[:, :, H // 8 : SUMMED // 4], parted(sums2[q]))
 
         c_cols = sb("c_cols", [P, 4 * T], BF16)
 
         def turn_back(q, b):
             turned = bank(b)
             for u in range(2):
-                nc.tensor.transpose(turned[:, u * P : (u + 1) * P], c_rows[q][:].bitcast(F32)[:, u * P : (u + 1) * P], ident[:])
+                nc.tensor.transpose(turned[:, u * P : (u + 1) * P], c_pairs[q // 2][:].bitcast(F32)[:, (q % 2 * 2 + u) * P : (q % 2 * 2 + u + 1) * P], ident[:])
             return turned
 
         def interleave(q, turned, copy):
@@ -303,20 +320,21 @@ def tile_moe_sdn_glu_relu_kernel(
 
         weigh_first(0)
         weigh_first(1)
-        leave_sums(0, on_scalar)
-        add_second(0)
-        add_second(1)
-        leave_sums(1, on_scalar)
+        leave01(0, on_scalar)
         weigh_first(2)
+        leave01(1, on_scalar)
         weigh_first(3)
-        leave_sums(2, on_scalar)
+        add_second(0)
+        leave2_pair(on_vector)
+        add_second(1)
         add_second(2)
+        leave2(2, on_vector)
+        leave2(3, on_vector)
         add_second(3)
-        leave_sums(3, on_vector)
-        turned = [turn_back(q, b) for q, b in enumerate((0, 1, 2, 3))]
+        turned = [turn_back(q, b) for q, b in enumerate((7, 5, 1, 2))]
         for q, copy in enumerate((on_scalar, on_vector, on_scalar, on_scalar)):
             interleave(q, turned[q], copy)
-        parts = ((0, 2, 5, on_vector), (2, 3, 4, on_vector), (3, 4, 6, on_scalar))
+        parts = ((0, 2, 4, on_scalar), (2, 3, 6, on_vector), (3, 4, 0, on_vector))
         results = [project(q0, q1, b) for q0, q1, b, copy in parts]
         for acc, (q0, q1, b, copy) in zip(results, parts):
             store(acc, q0, q1, copy)

@@ -165,14 +165,13 @@ def tile_moe_sdn_glu_relu_kernel(
         def entries_of(r, t0, t1):
             return pos_sb[r][:, t0 // 16 : t1 // 16]
 
-        def fetch_weighed(j, r, t0, t1):
+        def fetch(j, r, t0, t1):
             term = sb("term%d_%d_%d" % (j, r, t0), [P, t1 - t0], F32)
-            nc.vector.tensor_tensor(term[:], h[j][:].indirect(entries_of(r, t0, t1)), gate_rows[r][:, t0:t1], MULT)
-            return [term[:, at : at + P] for at in range(0, t1 - t0, P)]
-
-        def fetch_plain(j, r, t0, t1):
-            term = sb("term%d_%d_%d" % (j, r, t0), [P, t1 - t0], F32)
-            nc.scalar.activation(term[:], h[j][:].indirect(entries_of(r, t0, t1)), COPY)
+            window = h[j][:].indirect(entries_of(r, t0, t1))
+            if j in (0, 3):
+                nc.scalar.activation(term[:], window, COPY)
+            else:
+                nc.vector.tensor_copy(term[:], window)
             return term
 
         def turn(piece, into, start, stop):
@@ -191,67 +190,36 @@ def tile_moe_sdn_glu_relu_kernel(
         product1_third()
         unit(1, high[2:], 1, 3, sb("gated1_fourth", [P, GATHER], F32))()
 
-        terms0 = [fetch_plain(0, r, 0, T) for r in range(2)]
-        terms1 = [fetch_weighed(1, r, 0, T) for r in range(2)]
-        late_products = [
-            unit(3, low, 4, 5, on_hidden("gated3_low", 0), GATHER),
-            unit(3, high, 0, 2, on_hidden("gated3_high", 1), GATHER),
-            unit(2, high, 1, 3, on_hidden("gated2_high", 3), GATHER),
-        ]
-        weighed0 = [on_hidden("weighed_first", 2)]
-        nc.gpsimd.tensor_tensor(weighed0[0][:], terms0[0][:], gate_rows[0][:], MULT)
-        late_products[0]()
-        weighed0.append(on_hidden("weighed_second", 0))
-        nc.gpsimd.tensor_tensor(weighed0[1][:], terms0[1][:], gate_rows[1][:], MULT)
-        late_products[1]()
-        late_products[2]()
-        unit(2, low, 6, 7, on_hidden("gated2_low", 1), GATHER)()
+        early_terms = [[fetch(j, r, 0, T) for j in range(2)] for r in range(2)]
+        weighed = [[sb("weighed%d%d" % (r, j), [P, T], F32) for j in range(2)] for r in range(2)]
+        for r in range(2):
+            for j in range(2):
+                nc.gpsimd.tensor_tensor(weighed[r][j][:], early_terms[r][j][:], gate_rows[r][:], MULT)
+        unit(3, low, 4, 5, on_hidden("gated3_low", 0), GATHER)()
+        unit(3, high, 0, 2, on_hidden("gated3_high", 1), GATHER)()
+        unit(2, high, 1, 3, on_hidden("gated2_high", 3), GATHER)()
+        unit(2, low, 6, 7, on_hidden("gated2_low", 2), GATHER)()
 
-        first3 = fetch_plain(3, 0, 0, T)
-        second3 = [fetch_plain(3, 1, a * PAIR, (a + 1) * PAIR) for a in range(2)]
-        terms2 = [[], []]
-        for t0, t1 in ((0, PAIR), (PAIR, PAIR + P), (PAIR + P, T)):
-            for r in range(2):
-                terms2[r].extend(fetch_weighed(2, r, t0, t1))
+        late_terms = {(j, r, a): fetch(j, r, a * PAIR, (a + 1) * PAIR) for j in (3, 2) for a in range(2) for r in range(2)}
 
         sums01 = [bank(5), bank(2)]
+        for r in range(2):
+            for j in range(2):
+                for q in range(BLOCKS):
+                    at = (2 * j + q % 2) * P
+                    first, last = r == 0 and j == 0 and q % 2 == 0, r == 1 and j == 1 and q % 2 == 1
+                    turn(weighed[r][j][:, q * P : (q + 1) * P], sums01[q // 2][:, at : at + P], first, last)
 
-        def turn01(j, pieces, start, stop):
-            for q in range(BLOCKS):
-                at = (2 * j + q % 2) * P
-                turn(pieces[q], sums01[q // 2][:, at : at + P], start and q % 2 == 0, stop and q % 2 == 1)
-
-        def blocks_of(term):
-            return [term[:, q * P : (q + 1) * P] for q in range(BLOCKS)]
-
-        turn01(1, terms1[0], True, False)
-        turn01(1, terms1[1], False, False)
-        turn01(0, blocks_of(weighed0[0]), False, False)
-        turn01(0, blocks_of(weighed0[1]), False, True)
-        turned3 = [bank(4), bank(0)]
-        first_pair = bank(1)
-        sums2 = [first_pair[:, :P], first_pair[:, P:PAIR], bank(6)[:, :P], bank(3)[:, :P]]
-        for q in range(BLOCKS):
-            turn(first3[:, q * P : (q + 1) * P], turned3[0][:, q * P : (q + 1) * P], True, True)
-
-        def turn2(q):
-            for r in range(2):
-                turn(terms2[r][q], sums2[q], r == 0, r == 1)
-
-        def turn3(q):
-            turn(second3[q // 2][:, q % 2 * P : (q % 2 + 1) * P], turned3[1][:, q * P : (q + 1) * P], True, True)
-
-        turn2(0)
-        turn2(1)
-        turn3(0)
-        turn3(1)
-        turn2(2)
-        turn3(2)
-        turn3(3)
-        turn2(3)
+        turned23 = [[bank(4), bank(1)], [bank(0), bank(6)]]
+        for a in range(2):
+            for j in (3, 2):
+                for r in range(2):
+                    for q in range(2):
+                        at = (2 * q + j - 2) * P
+                        turn(late_terms[j, r, a][:, q * P : (q + 1) * P], turned23[r][a][:, at : at + P], True, True)
 
         c_pairs = [sb("c_pair%d" % a, [P, 2 * H], BF16) for a in range(2)]
-        firsts = [sb("first%d" % q, [P, P], F32) for q in range(BLOCKS)]
+        firsts = [sb("first%d" % q, [P, PAIR], F32) for q in range(BLOCKS)]
 
         def parted(cols):
             return cols.rearrange("t (p u e) -> t u p e", u=2, e=2)
@@ -259,14 +227,17 @@ def tile_moe_sdn_glu_relu_kernel(
         def rows_of(q):
             return c_pairs[q // 2][:, q % 2 * H : (q % 2 + 1) * H].rearrange("t (u p e) -> t u p e", u=2, e=2)
 
+        def block_of(r, q):
+            return turned23[r][q // 2][:, q % 2 * PAIR : (q % 2 + 1) * PAIR]
+
         def weigh_first(q):
-            nc.scalar.activation(firsts[q][:], turned3[0][:, q * P : (q + 1) * P], COPY, scale=gate_tok[0][:, q : q + 1])
+            nc.scalar.activation(firsts[q][:], block_of(0, q), COPY, scale=gate_tok[0][:, q : q + 1])
 
         def add_second(q):
             for u in range(2):
                 nc.vector.scalar_tensor_tensor(
-                    rows_of(q)[:, u, SUMMED // 4 :],
-                    parted(turned3[1][:, q * P : (q + 1) * P])[:, u],
+                    rows_of(q)[:, u, P // 2 :],
+                    parted(block_of(1, q))[:, u],
                     gate_tok[1][:, q : q + 1],
                     parted(firsts[q][:])[:, u],
                     MULT,
@@ -276,13 +247,6 @@ def tile_moe_sdn_glu_relu_kernel(
         def leave01(a, copy):
             rows = c_pairs[a][:].rearrange("t (q u j w) -> t j q u w", q=2, u=2, j=ROW_TILES)[:, :2]
             copy(rows, sums01[a][:].rearrange("t (jq p u e) -> t jq u p e", jq=4, u=2, e=2))
-
-        def leave2_pair(copy):
-            rows = c_pairs[0][:].rearrange("t (q u j w) -> t j q u w", q=2, u=2, j=ROW_TILES)[:, 2]
-            copy(rows, first_pair[:, :PAIR].rearrange("t (q p u e) -> t q u p e", q=2, u=2, e=2))
-
-        def leave2(q, copy):
-            copy(rows_of(q)[:, :, H // 8 : SUMMED // 4], parted(sums2[q]))
 
         c_cols = sb("c_cols", [P, 4 * T], BF16)
 
@@ -322,19 +286,16 @@ def tile_moe_sdn_glu_relu_kernel(
         weigh_first(1)
         leave01(0, on_scalar)
         weigh_first(2)
-        leave01(1, on_scalar)
         weigh_first(3)
         add_second(0)
-        leave2_pair(on_vector)
         add_second(1)
+        leave01(1, on_vector)
         add_second(2)
-        leave2(2, on_vector)
-        leave2(3, on_vector)
         add_second(3)
-        turned = [turn_back(q, b) for q, b in enumerate((7, 5, 1, 2))]
-        for q, copy in enumerate((on_scalar, on_vector, on_scalar, on_scalar)):
-            interleave(q, turned[q], copy)
-        parts = ((0, 2, 4, on_scalar), (2, 3, 6, on_vector), (3, 4, 0, on_vector))
+        turned = [turn_back(q, b) for q, b in enumerate((3, 7, 5, 4))]
+        for q in range(BLOCKS):
+            interleave(q, turned[q], on_scalar)
+        parts = ((0, 2, 0, on_vector), (2, 3, 2, on_vector), (3, 4, 1, on_scalar))
         results = [project(q0, q1, b) for q0, q1, b, copy in parts]
         for acc, (q0, q1, b, copy) in zip(results, parts):
             store(acc, q0, q1, copy)

@@ -165,10 +165,10 @@ def tile_moe_sdn_glu_relu_kernel(
         def entries_of(r, t0, t1):
             return pos_sb[r][:, t0 // 16 : t1 // 16]
 
-        def fetch(j, r, t0, t1):
+        def fetch(j, r, t0, t1, scalar):
             term = sb("term%d_%d_%d" % (j, r, t0), [P, t1 - t0], F32)
             window = h[j][:].indirect(entries_of(r, t0, t1))
-            if j in (0, 3):
+            if scalar:
                 nc.scalar.activation(term[:], window, COPY)
             else:
                 nc.vector.tensor_copy(term[:], window)
@@ -190,35 +190,45 @@ def tile_moe_sdn_glu_relu_kernel(
         product1_third()
         unit(1, high[2:], 1, 3, sb("gated1_fourth", [P, GATHER], F32))()
 
-        early_terms = [[fetch(j, r, 0, T) for j in range(2)] for r in range(2)]
-        weighed = [[sb("weighed%d%d" % (r, j), [P, T], F32) for j in range(2)] for r in range(2)]
+        weighed = {(0, 1): sb("weighed01", [P, T], F32)}
+        nc.vector.tensor_tensor(weighed[0, 1][:], h[1][:].indirect(pos_sb[0][:]), gate_rows[0][:], MULT)
+        plain = {(r, j): fetch(j, r, 0, T, j == 0) for r, j in ((0, 0), (1, 0), (1, 1))}
+
+        def weigh_rows(r, j, tile):
+            weighed[r, j] = tile
+            nc.gpsimd.tensor_tensor(tile[:], plain[r, j][:], gate_rows[r][:], MULT)
+
         for r in range(2):
-            for j in range(2):
-                nc.gpsimd.tensor_tensor(weighed[r][j][:], early_terms[r][j][:], gate_rows[r][:], MULT)
+            weigh_rows(r, 0, sb("weighed%d0" % r, [P, T], F32))
         unit(3, low, 4, 5, on_hidden("gated3_low", 0), GATHER)()
+        weigh_rows(1, 1, on_hidden("weighed11", 0))
         unit(3, high, 0, 2, on_hidden("gated3_high", 1), GATHER)()
         unit(2, high, 1, 3, on_hidden("gated2_high", 3), GATHER)()
         unit(2, low, 6, 7, on_hidden("gated2_low", 2), GATHER)()
 
-        late_terms = {(j, r, a): fetch(j, r, a * PAIR, (a + 1) * PAIR) for j in (3, 2) for a in range(2) for r in range(2)}
+        late_terms = {}
+        cuts = [(j, r, 2 * a, 2 * a + 2, a == 0) for a in range(2) for r in range(2) for j in (3, 2)]
+        for j, r, q0, q1, scalar in cuts:
+            term = fetch(j, r, q0 * P, q1 * P, scalar)
+            for q in range(q0, q1):
+                late_terms[j, r, q] = term[:, (q - q0) * P : (q - q0 + 1) * P]
 
         sums01 = [bank(5), bank(2)]
-        for r in range(2):
-            for j in range(2):
-                for q in range(BLOCKS):
-                    at = (2 * j + q % 2) * P
-                    first, last = r == 0 and j == 0 and q % 2 == 0, r == 1 and j == 1 and q % 2 == 1
-                    turn(weighed[r][j][:, q * P : (q + 1) * P], sums01[q // 2][:, at : at + P], first, last)
+        for r, j in ((0, 1), (0, 0), (1, 0), (1, 1)):
+            for q in range(BLOCKS):
+                at = (2 * j + q % 2) * P
+                first, last = r == 0 and j == 1 and q % 2 == 0, r == 1 and j == 1 and q % 2 == 1
+                turn(weighed[r, j][:, q * P : (q + 1) * P], sums01[q // 2][:, at : at + P], first, last)
 
         turned23 = [[bank(4), bank(1)], [bank(0), bank(6)]]
-        for a in range(2):
+        for r in range(2):
             for j in (3, 2):
-                for r in range(2):
+                for a in range(2):
                     for q in range(2):
                         at = (2 * q + j - 2) * P
-                        turn(late_terms[j, r, a][:, q * P : (q + 1) * P], turned23[r][a][:, at : at + P], True, True)
+                        turn(late_terms[j, r, 2 * a + q], turned23[r][a][:, at : at + P], True, True)
 
-        c_pairs = [sb("c_pair%d" % a, [P, 2 * H], BF16) for a in range(2)]
+        c_pairs = [hidden.tile([P, 2 * H], BF16, name="c_pair%d" % a, offset=(3 - a) * H_BYTES) for a in range(2)]
         firsts = [sb("first%d" % q, [P, PAIR], F32) for q in range(BLOCKS)]
 
         def parted(cols):
@@ -282,20 +292,15 @@ def tile_moe_sdn_glu_relu_kernel(
             copy(result[:], acc)
             nc.sync.dma_start(out[:, q0 * P : q1 * P], result[:])
 
-        weigh_first(0)
-        weigh_first(1)
         leave01(0, on_scalar)
-        weigh_first(2)
-        weigh_first(3)
-        add_second(0)
-        add_second(1)
         leave01(1, on_vector)
-        add_second(2)
-        add_second(3)
-        turned = [turn_back(q, b) for q, b in enumerate((3, 7, 5, 4))]
         for q in range(BLOCKS):
-            interleave(q, turned[q], on_scalar)
-        parts = ((0, 2, 0, on_vector), (2, 3, 2, on_vector), (3, 4, 1, on_scalar))
+            weigh_first(q)
+            add_second(q)
+        turned = [turn_back(q, b) for q, b in enumerate((3, 7, 5, 4))]
+        for q, copy in enumerate((on_scalar, on_scalar, on_scalar, on_scalar)):
+            interleave(q, turned[q], copy)
+        parts = ((0, 2, 0, on_scalar), (2, 3, 2, on_vector), (3, 4, 1, on_vector))
         results = [project(q0, q1, b) for q0, q1, b, copy in parts]
         for acc, (q0, q1, b, copy) in zip(results, parts):
             store(acc, q0, q1, copy)

from contextlib import ExitStack

import concourse.mybir as mybir
from concourse.masks import make_identity

K, T, E, C, H, N = 512, 512, 8, 128, 512, 128
FLOPS = 2 * (2 * K * H * E * C + H * N * T)

F32 = mybir.dt.float32
BF16 = mybir.dt.bfloat16
I32 = mybir.dt.int32
U32 = mybir.dt.uint32
U16 = mybir.dt.uint16
U8 = mybir.dt.uint8
FP8X4 = mybir.dt.float8_e4m3fn_x4
FP4X4 = mybir.dt.float4_e2m1fn_x4
MULT = mybir.AluOpType.mult
ADD = mybir.AluOpType.add
RELU = mybir.ActivationFunctionType.Relu
COPY = mybir.ActivationFunctionType.Copy

P = 128
BANK = 512
SLOTS = E * C
GROUP = 4
GROUPS = E // GROUP
GROUP_SLOTS = GROUP * C
ROW_TILES = H // P
BLOCKS = T // P
PAIR = 2 * P
GATHER = 2 * C
HALF_ROW = H
EARLY_LOADS = ((0, 4), (4, 6), (6, 8))
H_BYTES = 4 * SLOTS
SUMMED = 3 * P


def tile_moe_sdn_glu_relu_kernel(
    tc, x_words, x_scales, w1_words, w1_scales, w3_words, w3_scales, w2_words, w2_scales, gate, offs, pos1, pos2, out
):
    nc = tc.nc
    with ExitStack() as ctx:
        keep = ctx.enter_context(tc.tile_pool(name="keep", bufs=1))
        hidden = ctx.enter_context(tc.tile_pool(name="hidden", bufs=1))
        shared = ctx.enter_context(tc.tile_pool(name="shared", bufs=1))
        psum = ctx.enter_context(tc.psum_pool(name="psum", bufs=1))
        on_scalar, on_vector = nc.scalar.copy, nc.vector.tensor_copy

        def sb(name, shape, dtype):
            return keep.tile(shape, dtype, name=name, align_bytes=64)

        def bank(b):
            return psum.tile([P, BANK], F32, name="bank%d" % b)

        offs_sb = keep.tile([P, SLOTS // 16], U16, name="offs_sb")
        pos_sb = [keep.tile([P, T // 16], U16, name="pos%d_sb" % r) for r in range(2)]
        xw = sb("xw", [P, T], I32)
        xs = sb("xs", [P, T], U8)
        ws = [[sb("ws%d%d" % (m, a), [P, E, H // 2], U8) for a in range(2)] for m in range(2)]
        w2s = sb("w2s", [P, N], U8)
        w2w = sb("w2w", [P, 4 * N], U8)
        gate_rows = [sb("gate_rows%d" % r, [P, T], F32) for r in range(2)]
        gate_runs = shared.tile([P, 2, BLOCKS], F32, name="gate_runs", align_bytes=64, offset=0)
        gate_tok = [sb("gate_tok%d" % r, [P, BLOCKS], F32) for r in range(2)]
        ident = sb("ident", [P, P], F32)

        def load_scales(plane, rows, queues=(nc.sync,) * 4):
            for r, queue in enumerate(queues):
                queue.dma_start(plane[r:P:32], rows[r:16:4])

        w_words = [w.rearrange("e s p n -> p (e s) n").bitcast(I32) for w in (w1_words, w3_words)]
        w_scales = [w.rearrange("e s b n -> b (e s) n").bitcast(I32) for w in (w1_scales, w3_scales)]
        early = [[sb("we%d%d" % (m, e0), [P, e1 - e0, HALF_ROW], U8) for e0, e1 in EARLY_LOADS] for m in range(2)]
        late = [[sb("wl%d%d" % (m, g), [P, GROUP, HALF_ROW], U8) for g in range(GROUPS)] for m in range(2)]
        first_words, last_words = slice(0, HALF_ROW // 4), slice(HALF_ROW // 4, HALF_ROW // 2)
        first_scales, last_scales = slice(0, H // 8), slice(H // 8, H // 4)

        nc.vector.memset(xs[:].bitcast(I32), 0)
        make_identity(nc, ident[:])
        nc.sync.dma_start(xw[:], x_words[0].rearrange("p t d -> p (t d)").bitcast(I32))
        nc.sync.dma_start(offs_sb[:], offs)
        load_scales(xs[:].bitcast(I32), x_scales[0].bitcast(I32), (nc.sync, nc.scalar) * 2)
        nc.sync.dma_start(gate_runs[:], gate[:, 0].rearrange("r (p n) -> p r n", n=BLOCKS))
        for m in range(2):
            nc.sync.dma_start(early[m][0][:].bitcast(I32), w_words[m][:, 0:GROUP, first_words])
            load_scales(ws[m][0][:].bitcast(I32), w_scales[m][:, :, first_scales])
        for at, (e0, e1) in list(enumerate(EARLY_LOADS))[1:]:
            for m in range(2):
                nc.sync.dma_start(early[m][at][:].bitcast(I32), w_words[m][:, e0:e1, first_words])
        nc.sync.dma_start(pos_sb[0][:], pos1)
        nc.sync.dma_start(pos_sb[1][:], pos2)
        for m in range(2):
            nc.sync.dma_start(late[m][0][:].bitcast(I32), w_words[m][:, 0:GROUP, last_words])
            load_scales(ws[m][1][:].bitcast(I32), w_scales[m][:, :, last_scales])
            nc.sync.dma_start(late[m][1][:].bitcast(I32), w_words[m][:, GROUP:E, last_words])
        with nc.allow_non_contiguous_dma(reason="one gate value a token and partition"):
            for r in range(2):
                nc.sync.dma_start(gate_tok[r][:], gate[r, 0].rearrange("(q p) -> p q", p=P))
        nc.sync.dma_start(w2w[:].bitcast(I32), w2_words[0].rearrange("p n d -> p (n d)").bitcast(I32))
        load_scales(w2s[:].bitcast(I32), w2_scales[0].bitcast(I32))

        for r in range(2):
            spread = bank(7 - r)
            for n in range(BLOCKS):
                column = gate_runs[:, r, n : n + 1]
                nc.tensor.transpose(spread[:, n * P : (n + 1) * P], column.to_broadcast([P, P]), ident[:])
            nc.scalar.activation(
                gate_rows[r][:].rearrange("p (c n) -> p c n", n=BLOCKS), spread[:].rearrange("p (n c) -> p c n", n=BLOCKS), COPY
            )

        xg = [sb("xg0", [P, GROUP_SLOTS], U32), shared.tile([P, GROUP_SLOTS], U32, name="xg1", align_bytes=64, offset=0)]
        sg = [sb("sg%d" % g, [P, GROUP_SLOTS], U8) for g in range(GROUPS)]
        for g in range(GROUPS):
            for start in range(0, GROUP_SLOTS, GATHER):
                entries = offs_sb[:, (g * GROUP_SLOTS + start) // 16 : (g * GROUP_SLOTS + start + GATHER) // 16]
                nc.vector.tensor_copy(xg[g][:, start : start + GATHER], xw[:].bitcast(U32).indirect(entries))
                nc.vector.tensor_copy(sg[g][:, start : start + GATHER], xs[:].indirect(entries))

        h = [hidden.tile([P, SLOTS], F32, name="h%d" % j, offset=j * H_BYTES) for j in range(ROW_TILES)]

        def passes(m, j, experts, b):
            sums = bank(b)
            for at, e in enumerate(experts):
                g, el = divmod(e, GROUP)
                if j < 2:
                    load = max(e // 2 - 1, 0)
                    row = early[m][load][:, e - EARLY_LOADS[load][0]]
                else:
                    row = late[m][g][:, el]
                words = row[:, 2 * P * (j % 2) : 2 * P * (j % 2 + 1)]
                slots = slice(el * C, (el + 1) * C)
                nc.tensor.matmul_mx(
                    out=sums[:, at * C : (at + 1) * C],
                    lhsT=words.bitcast(FP4X4),
                    lhsT_scale=ws[m][j // 2][:, e, P * (j % 2) : P * (j % 2 + 1)],
                    rhs=xg[g][:, slots].bitcast(FP8X4),
                    rhs_scale=sg[g][:, slots],
                    start=True,
                    stop=True,
                )
            return sums[:, : len(experts) * C]

        def leave(sums, name, func):
            kept = sb(name, [P, sums.shape[1]], F32)
            nc.scalar.activation(kept[:], sums, func)
            return kept[:]

        def on_hidden(name, at):
            return hidden.tile([P, T], F32, name=name, offset=at * H_BYTES // 2)

        def unit(j, experts, bank_w1, bank_w3, gated, step=GROUP_SLOTS):
            sums = passes(0, j, experts, bank_w1)
            width = sums.shape[1]
            pieces = [slice(at, min(at + step, width)) for at in range(0, width, step)]
            for piece in pieces:
                nc.scalar.activation(gated[:, piece], sums[:, piece], RELU)
            linear = passes(1, j, experts, bank_w3)

            def multiply():
                for piece in pieces:
                    nc.vector.tensor_tensor(h[j][:, experts[0] * C :][:, piece], linear[:, piece], gated[:, piece], MULT)

            return multiply

        def entries_of(r, t0, t1):
            return pos_sb[r][:, t0 // 16 : t1 // 16]

        def fetch(j, r, t0, t1, scalar):
            term = sb("term%d_%d_%d" % (j, r, t0), [P, t1 - t0], F32)
            window = h[j][:].indirect(entries_of(r, t0, t1))
            if scalar:
                nc.scalar.activation(term[:], window, COPY)
            else:
                nc.vector.tensor_copy(term[:], window)
            return term

        def turn(piece, into, start, stop):
            nc.tensor.matmul(into, lhsT=piece, rhs=ident[:], is_transpose=True, start=start, stop=stop)

        low, high = range(0, GROUP), range(GROUP, E)
        gated = leave(passes(0, 0, low, 0), "gated0_low", RELU)
        for pair, b in enumerate((2, 7)):
            linear = leave(passes(1, 0, low[2 * pair : 2 * pair + 2], b), "linear0_%d" % pair, COPY)
            slots = slice(2 * pair * C, (2 * pair + 2) * C)
            nc.gpsimd.tensor_tensor(h[0][:, slots], linear, gated[:, slots], MULT)
        unit(1, low, 1, 3, sb("gated1_low", [P, GROUP_SLOTS], F32))()
        unit(0, high[:2], 4, 5, sb("gated0_third", [P, GATHER], F32))()
        product1_third = unit(1, high[:2], 0, 2, sb("gated1_third", [P, GATHER], F32))
        unit(0, high[2:], 6, 7, sb("gated0_fourth", [P, GATHER], F32))()
        product1_third()
        unit(1, high[2:], 1, 3, sb("gated1_fourth", [P, GATHER], F32))()

        weighed = {(0, 1): sb("weighed01", [P, T], F32)}
        nc.vector.tensor_tensor(weighed[0, 1][:], h[1][:].indirect(pos_sb[0][:]), gate_rows[0][:], MULT)
        plain = {(r, j): fetch(j, r, 0, T, j == 0) for r, j in ((0, 0), (1, 0), (1, 1))}

        def weigh_rows(r, j, tile):
            weighed[r, j] = tile
            nc.gpsimd.tensor_tensor(tile[:], plain[r, j][:], gate_rows[r][:], MULT)

        for r in range(2):
            weigh_rows(r, 0, sb("weighed%d0" % r, [P, T], F32))
        unit(3, low, 4, 5, on_hidden("gated3_low", 0), GATHER)()
        weigh_rows(1, 1, on_hidden("weighed11", 0))
        unit(3, high, 0, 2, on_hidden("gated3_high", 1), GATHER)()
        unit(2, high, 1, 3, on_hidden("gated2_high", 3), GATHER)()
        unit(2, low, 6, 7, on_hidden("gated2_low", 2), GATHER)()

        late_terms = {}
        cuts = [(j, r, 2 * a, 2 * a + 2, a == 0) for a in range(2) for r in range(2) for j in (3, 2)]
        for j, r, q0, q1, scalar in cuts:
            term = fetch(j, r, q0 * P, q1 * P, scalar)
            for q in range(q0, q1):
                late_terms[j, r, q] = term[:, (q - q0) * P : (q - q0 + 1) * P]

        sums01 = [bank(5), bank(2)]
        for r, j in ((0, 1), (0, 0), (1, 0), (1, 1)):
            for q in range(BLOCKS):
                at = (2 * j + q % 2) * P
                first, last = r == 0 and j == 1 and q % 2 == 0, r == 1 and j == 1 and q % 2 == 1
                turn(weighed[r, j][:, q * P : (q + 1) * P], sums01[q // 2][:, at : at + P], first, last)

        turned23 = [[bank(4), bank(1)], [bank(0), bank(6)]]
        for r in range(2):
            for j in (3, 2):
                for a in range(2):
                    for q in range(2):
                        at = (2 * q + j - 2) * P
                        turn(late_terms[j, r, 2 * a + q], turned23[r][a][:, at : at + P], True, True)

        c_pairs = [hidden.tile([P, 2 * H], BF16, name="c_pair%d" % a, offset=(3 - a) * H_BYTES) for a in range(2)]
        firsts = [sb("first%d" % q, [P, PAIR], F32) for q in range(BLOCKS)]

        def parted(cols):
            return cols.rearrange("t (p u e) -> t u p e", u=2, e=2)

        def rows_of(q):
            return c_pairs[q // 2][:, q % 2 * H : (q % 2 + 1) * H].rearrange("t (u p e) -> t u p e", u=2, e=2)

        def block_of(r, q):
            return turned23[r][q // 2][:, q % 2 * PAIR : (q % 2 + 1) * PAIR]

        def weigh_first(q):
            nc.scalar.activation(firsts[q][:], block_of(0, q), COPY, scale=gate_tok[0][:, q : q + 1])

        def add_second(q):
            for u in range(2):
                nc.vector.scalar_tensor_tensor(
                    rows_of(q)[:, u, P // 2 :],
                    parted(block_of(1, q))[:, u],
                    gate_tok[1][:, q : q + 1],
                    parted(firsts[q][:])[:, u],
                    MULT,
                    ADD,
                )

        def leave01(a, copy):
            rows = c_pairs[a][:].rearrange("t (q u j w) -> t j q u w", q=2, u=2, j=ROW_TILES)[:, :2]
            copy(rows, sums01[a][:].rearrange("t (jq p u e) -> t jq u p e", jq=4, u=2, e=2))

        c_cols = sb("c_cols", [P, 4 * T], BF16)

        def turn_back(q, b):
            turned = bank(b)
            for u in range(2):
                nc.tensor.transpose(turned[:, u * P : (u + 1) * P], c_pairs[q // 2][:].bitcast(F32)[:, (q % 2 * 2 + u) * P : (q % 2 * 2 + u + 1) * P], ident[:])
            return turned

        def interleave(q, turned, copy):
            words = c_cols[:].bitcast(F32)[:, q * PAIR : (q + 1) * PAIR]
            copy(words.rearrange("p (t u) -> p t u", u=2), turned[:, :PAIR].rearrange("p (u t) -> p t u", u=2))

        def project(q0, q1, b):
            width = (q1 - q0) * P
            codes = sb("codes%d" % q0, [P, width], U32)
            scales = sb("scales%d" % q0, [P, width], U8)
            nc.vector.quantize_mx(out=codes[:].bitcast(FP8X4), scales=scales[:], in_=c_cols[:, 4 * P * q0 : 4 * P * q1])
            acc = bank(b)
            nc.tensor.matmul_mx(
                out=acc[:, :width],
                lhsT=w2w[:].bitcast(FP8X4),
                lhsT_scale=w2s[:],
                rhs=codes[:].bitcast(FP8X4),
                rhs_scale=scales[:],
                start=True,
                stop=True,
            )
            return acc[:, :width]

        def store(acc, q0, q1, copy):
            result = sb("result%d" % q0, [P, (q1 - q0) * P], F32)
            copy(result[:], acc)
            nc.sync.dma_start(out[:, q0 * P : q1 * P], result[:])

        leave01(0, on_scalar)
        leave01(1, on_vector)
        for q in range(BLOCKS):
            weigh_first(q)
            add_second(q)
        turned = [turn_back(q, b) for q, b in enumerate((3, 7, 5, 4))]
        for q, copy in enumerate((on_scalar, on_scalar, on_scalar, on_scalar)):
            interleave(q, turned[q], copy)
        parts = ((0, 2, 0, on_scalar), (2, 3, 2, on_vector), (3, 4, 1, on_vector))
        results = [project(q0, q1, b) for q0, q1, b, copy in parts]
        for acc, (q0, q1, b, copy) in zip(results, parts):
            store(acc, q0, q1, copy)
